import numpy as np
import ml_dtypes


def mxq(x, axis, fmt="e4m3"):
    dtype, down = {"e4m3": (ml_dtypes.float8_e4m3fn, 7), "e5m2": (ml_dtypes.float8_e5m2, 14)}[fmt]
    v = np.moveaxis(np.asarray(x, np.float32).astype(ml_dtypes.bfloat16).astype(np.float64), axis, -1)
    blocks = v.reshape(v.shape[:-1] + (-1, 32))
    amax = np.abs(blocks).max(-1, keepdims=True)
    byte = np.maximum(np.where(amax > 0, np.frexp(amax)[1] - 1 + 127, 0) - down, 1)
    scale = np.exp2(byte - 127.0)
    codes = (blocks / scale).astype(np.float32).astype(dtype).astype(np.float64)
    return np.moveaxis((codes * scale).reshape(v.shape), -1, axis)


WIDE = False


def mx_kscale(k):
    if not WIDE:
        return np.ones(k)
    levels = np.array([10, -10, 5, -5, 0])
    if k % 512:
        return np.exp2(np.random.permutation(np.resize(levels, k // 32))).repeat(32)
    a = np.empty((k // 512, 16))
    for p in range(k // 512):
        a[p, :8] = np.random.permutation(np.resize(levels, 8))
        for g in range(8):
            far = levels[np.abs(levels - a[p, g]) >= 10]
            a[p, g + 8] = far[np.random.randint(len(far))]
    return np.exp2(a.ravel()).repeat(32)


def f64(x):
    return np.asarray(x).astype(np.float64)


def striped(idx):
    return np.tile(idx.reshape(-1, 16).T, (8, 1)).astype(np.uint16)


def unstriped(offs):
    return offs[:16].T.reshape(-1).astype(np.int64)


E2M1 = np.array([0.0, 0.5, 1.0, 1.5, 2.0, 3.0, 4.0, 6.0, -0.0, -0.5, -1.0, -1.5, -2.0, -3.0, -4.0, -6.0])


def pack_weight(w, fmt):
    k, n = w.shape
    w = f64(np.asarray(w, np.float32).astype(ml_dtypes.bfloat16)).reshape(k // 32, 32, n)
    amax = np.abs(w).max(1)
    if fmt == "e4m3":
        byte = np.frexp(amax)[1] - 1 + 127 - 7
    else:
        mant, ex = np.frexp(amax / 6.0)
        byte = np.where(mant > 0.5, ex, ex - 1) + 127
    byte = np.clip(np.where(amax > 0, byte, 1), 1, 254)
    scaled = (w * np.exp2(127.0 - byte)[:, None, :]).reshape(k, n).astype(np.float32)
    by_word = np.ascontiguousarray(scaled.reshape(k // 512, 128, 4, n).transpose(0, 1, 3, 2))
    if fmt == "e4m3":
        words = by_word.astype(ml_dtypes.float8_e4m3fn).view(np.uint8)
    else:
        c = by_word.astype(ml_dtypes.float4_e2m1fn).view(np.uint8) & 0xF
        words = (c[..., 0::2] | (c[..., 1::2] << 4)).reshape(k // 512, 128, 2 * n)
    return np.ascontiguousarray(words), np.ascontiguousarray(byte.astype(np.uint8).reshape(k // 512, 16, n))


def unpack_weight(words, scales, fmt):
    g, _, n = scales.shape
    words = np.ascontiguousarray(words).reshape(g, 128, n, -1)
    if fmt == "e4m3":
        vals = words.view(ml_dtypes.float8_e4m3fn).astype(np.float64)
    else:
        nib = np.empty((g, 128, n, 4), np.uint8)
        nib[..., 0::2] = words & 0xF
        nib[..., 1::2] = words >> 4
        vals = E2M1[nib]
    vals = vals * np.repeat(np.exp2(scales.astype(np.float64) - 127.0), 8, axis=1)[..., None]
    return vals.transpose(0, 1, 3, 2).reshape(g * 512, n)


def gelu(v):
    return 0.5 * v * (1.0 + np.tanh(np.sqrt(2.0 / np.pi) * (v + 0.044715 * v**3)))


K, M, H, N, T, T2, S = 512, 1024, 1024, 512, 2048, 4096, 1024

def setup_inputs():
    n = np.random.standard_normal
    s, s2, u = mx_kscale(K)[:, None], mx_kscale(M)[:, None], mx_kscale(H)[:, None]
    tab_words, tab_scales = pack_weight(n((K, T)) * s, "e4m3")
    tab2_words, tab2_scales = pack_weight(n((M, T2)) * s2, "e4m3")
    w4_words, w4_scales = pack_weight(n((H, N)) / np.sqrt(H) / u, "e2m1")
    return {
        "tab_words": tab_words, "tab_scales": tab_scales,
        "offs": striped(np.random.permutation(T)[:S]),
        "tab2_words": tab2_words, "tab2_scales": tab2_scales,
        "offs2": striped(np.random.permutation(T2)[:S]),
        "w1": (0.4 * n((K, H)) / np.sqrt(K) / s).astype(np.float32),
        "b1": (0.3 * n(H) - 0.5).astype(np.float32),
        "w2": (n((M, H)) / np.sqrt(M) / s2 * u.T).astype(np.float32),
        "w4_words": w4_words, "w4_scales": w4_scales,
        "fx": np.exp(0.2 * n(N)).astype(np.float32),
    }

def reference(tab_words, tab_scales, offs, tab2_words, tab2_scales, offs2, w1, b1, w2, w4_words, w4_scales, fx):
    v = unpack_weight(tab_words, tab_scales, "e4m3")[:, unstriped(offs)]
    v2 = unpack_weight(tab2_words, tab2_scales, "e4m3")[:, unstriped(offs2)]
    w1q = mxq(f64(w1), 0, "e4m3")
    w2q = mxq(f64(w2), 0, "e4m3")
    w4 = unpack_weight(w4_words, w4_scales, "e2m1")
    l = (w1q.T @ v) + f64(b1)[:, None]
    c = w2q.T @ v2
    h = np.exp(l) * c
    hq = mxq(h, 0, "e4m3")
    y = w4.T @ hq
    return f64(fx)[:, None] * y

@@ -1,0 +1,262 @@
+from contextlib import ExitStack
+
+import concourse.mybir as mybir
+
+K, M, H, N, T, T2, S = 512, 1024, 1024, 512, 2048, 4096, 1024
+FLOPS = 2 * S * (K * H + M * H + H * N)
+
+F32 = mybir.dt.float32
+BF16 = mybir.dt.bfloat16
+I32 = mybir.dt.int32
+U32 = mybir.dt.uint32
+U16 = mybir.dt.uint16
+U8 = mybir.dt.uint8
+FP8X4 = mybir.dt.float8_e4m3fn_x4
+FP4X4 = mybir.dt.float4_e2m1fn_x4
+EXP = mybir.ActivationFunctionType.Exp
+COPY = mybir.ActivationFunctionType.Copy
+MULT = mybir.AluOpType.mult
+
+P = 128
+PACK = 4
+KP = P * PACK
+HALF = 512
+CH = 128
+NCH = S // CH
+LIST_COLS = S // 16
+
+
+def tile_list_scenario_cashflow_values_kernel(
+    tc, tab_words, tab_scales, offs, tab2_words, tab2_scales, offs2, w1, b1, w2, w4_words, w4_scales, fx, out
+):
+    nc = tc.nc
+    with ExitStack() as ctx:
+        keep = ctx.enter_context(tc.tile_pool(name="keep", bufs=1))
+        ring = ctx.enter_context(tc.tile_pool(name="ring", bufs=3))
+        psum = ctx.enter_context(tc.psum_pool(name="psum", bufs=4))
+
+        def kept(shape, dtype, name):
+            return keep.tile(shape, dtype, name=name, align_bytes=64)
+
+        idx = kept([P, LIST_COLS], U16, "idx")
+        idx2 = kept([P, LIST_COLS], U16, "idx2")
+        curve_words = kept([P, T], I32, "curve_words")
+        curve_scales = kept([P, T // 4], I32, "curve_scales")
+        cash_words = [kept([P, T2], I32, f"cash_words{a}") for a in range(2)]
+        cash_scales = kept([P, T2 // 4], I32, "cash_scales")
+        shift_words = kept([P, 2, 2 * N // 4], I32, "shift_words")
+        shift_scales = kept([P, 2, N // 4], I32, "shift_scales")
+        bias = kept([P, 2, PACK], F32, "bias")
+        rate = kept([P, N // P], F32, "rate")
+        v_words = kept([P, S], U32, "v_words")
+        v_scales = kept([P, S], U8, "v_scales")
+        v2_words = [kept([P, S], U32, f"v2_words{a}") for a in range(2)]
+        v2_scales = kept([P, S], U8, "v2_scales")
+
+        pieces = {
+            "w1_0": (w1, 0, 0), "w1_1": (w1, 0, 1),
+            "w2_00": (w2, 0, 0), "w2_01": (w2, 1, 0), "w2_10": (w2, 0, 1), "w2_11": (w2, 1, 1),
+        }
+        raw = {name: kept([P, PACK, KP], F32, "raw_" + name) for name in pieces}
+        w_codes = {name: kept([P, KP], U32, "codes_" + name) for name in pieces}
+        w_scales = {name: kept([P, KP], U8, "scales_" + name) for name in pieces}
+        disc = {(a, hf): kept([P, PACK, HALF], F32, f"disc{a}{hf}") for a in range(2) for hf in range(2)}
+        h_codes = {(a, hf): kept([P, HALF], U32, f"h_codes{a}{hf}") for a in range(2) for hf in range(2)}
+        h_scales = {(a, hf): kept([P, HALF], U8, f"h_scales{a}{hf}") for a in range(2) for hf in range(2)}
+
+        nc.gpsimd.memset(curve_scales[:], 0)
+        nc.vector.memset(cash_scales[:], 0)
+        nc.vector.memset(shift_scales[:], 0)
+
+        def load_cash_scales(g):
+            for q in range(4):
+                p0 = 32 * q + 4 + 4 * g
+                nc.sync.dma_start(out=cash_scales[p0 : p0 + 4, :], in_=tab2_scales[g, 4 * q : 4 * q + 4, :].bitcast(I32))
+
+        def load_piece(name, c0=0, c1=KP):
+            w, g, a = pieces[name]
+            src = w[g * KP : (g + 1) * KP, a * KP + c0 : a * KP + c1]
+            nc.sync.dma_start(out=raw[name][:, :, c0:c1], in_=src.rearrange("(p j) c -> p j c", j=PACK))
+
+        def load_words(tile, words, c0=0, c1=None):
+            nc.sync.dma_start(out=tile[:, c0:c1], in_=words.rearrange("p t i -> p (t i)").bitcast(I32)[:, c0:c1])
+
+        nc.sync.dma_start(idx[:], offs)
+        nc.sync.dma_start(idx2[:], offs2)
+        nc.sync.dma_start(out=bias[:], in_=b1.rearrange("(a p t) -> p a t", a=2, t=PACK))
+        with nc.allow_non_contiguous_dma(reason="one rate to a partition and output tile"):
+            nc.sync.dma_start(out=rate[:], in_=fx.rearrange("(u p) -> p u", p=P))
+        for q in range(4):
+            nc.sync.dma_start(out=curve_scales[32 * q : 32 * q + 4, :], in_=tab_scales[0, 4 * q : 4 * q + 4, :].bitcast(I32))
+        load_words(curve_words, tab_words[0], 0, T // 2)
+        load_words(curve_words, tab_words[0], T // 2, T)
+        load_piece("w1_0", 0, KP // 2)
+        load_piece("w1_0", KP // 2, KP)
+        load_words(cash_words[0], tab2_words[0])
+        load_cash_scales(0)
+        load_piece("w2_00")
+        load_cash_scales(1)
+        load_piece("w1_1")
+        load_piece("w2_01")
+        load_words(cash_words[1], tab2_words[1])
+        load_piece("w2_10")
+        load_piece("w2_11", 0, KP // 2)
+        load_piece("w2_11", KP // 2, KP)
+        nc.sync.dma_start(out=shift_words[:], in_=w4_words.bitcast(I32).rearrange("a p n -> p a n"))
+        for q in range(4):
+            nc.sync.dma_start(
+                out=shift_scales[32 * q : 32 * q + 4, :, :],
+                in_=w4_scales[:, 4 * q : 4 * q + 4, :].bitcast(I32).rearrange("a r n -> r a n"),
+            )
+
+        def gather(dst, window, lst, j0, j1):
+            nc.vector.tensor_copy(dst[:, j0:j1], window.indirect(lst[:, j0 // 16 : j1 // 16]))
+
+        rounded = {}
+
+        def round_piece(name, copy, cuts=(0, KP)):
+            grouped = ring.tile([P, PACK, P, PACK], BF16, name="grouped", align_bytes=64)
+            for c0, c1 in zip(cuts[:-1], cuts[1:]):
+                copy(
+                    out=grouped[:, :, c0 // PACK : c1 // PACK, :].rearrange("p t m j -> p m j t"),
+                    in_=raw[name][:, :, c0:c1].rearrange("p j (m t) -> p m j t", t=PACK),
+                )
+            rounded[name] = grouped
+
+        def quantize_piece(name):
+            nc.vector.quantize_mx(
+                out=w_codes[name][:].bitcast(FP8X4),
+                scales=w_scales[name][:],
+                in_=rounded[name][:].rearrange("p t m j -> p (t m j)"),
+            )
+
+        def discount(a, hf):
+            name = f"w1_{a}"
+            cols = slice(hf * HALF, (hf + 1) * HALF)
+            for t in range(PACK):
+                bank = psum.tile([P, HALF], F32, name="wide")
+                nc.tensor.matmul_mx(
+                    out=bank[:],
+                    lhsT=w_codes[name][:, t * P : (t + 1) * P].bitcast(FP8X4),
+                    lhsT_scale=w_scales[name][:, t * P : (t + 1) * P],
+                    rhs=v_words[:, cols].bitcast(FP8X4),
+                    rhs_scale=v_scales[:, cols],
+                    start=True,
+                    stop=True,
+                )
+                nc.scalar.activation(out=disc[a, hf][:, t, :], in_=bank[:], func=EXP, bias=bias[:, a, t : t + 1])
+
+        values = {}
+
+        def present_value(a, ch):
+            cols = slice(ch * CH, (ch + 1) * CH)
+            bank = psum.tile([P, PACK, CH], F32, name="narrow")
+            for t in range(PACK):
+                for g in range(2):
+                    name = f"w2_{a}{g}"
+                    nc.tensor.matmul_mx(
+                        out=bank[:, t, :],
+                        lhsT=w_codes[name][:, t * P : (t + 1) * P].bitcast(FP8X4),
+                        lhsT_scale=w_scales[name][:, t * P : (t + 1) * P],
+                        rhs=v2_words[g][:, cols].bitcast(FP8X4),
+                        rhs_scale=v2_scales[4 + 4 * g : P, cols],
+                        start=(g == 0),
+                        stop=(g == 1),
+                    )
+            hf, j0 = divmod(ch * CH, HALF)
+            value = ring.tile([P, CH, PACK], BF16, name="value", align_bytes=64)
+            nc.vector.tensor_tensor(
+                out=value[:].rearrange("p (c i) t -> p c t i", i=4),
+                in0=bank[:].rearrange("p t (c i) -> p c t i", i=4),
+                in1=disc[a, hf][:, :, j0 : j0 + CH].rearrange("p t (c i) -> p c t i", i=4),
+                op=MULT,
+            )
+            values[a, ch] = value
+
+        def quantize_value(a, ch):
+            hf, j0 = divmod(ch * CH, HALF)
+            nc.vector.quantize_mx(
+                out=h_codes[a, hf][:, j0 : j0 + CH].bitcast(FP8X4),
+                scales=h_scales[a, hf][:, j0 : j0 + CH],
+                in_=values[a, ch][:].rearrange("p j t -> p (j t)"),
+            )
+
+        def scenario_pass(dst, u, a, hf, j0, j1):
+            nc.tensor.matmul_mx(
+                out=dst,
+                lhsT=shift_words[:, a, :].bitcast(U8)[:, 2 * P * u : 2 * P * (u + 1)].bitcast(FP4X4),
+                lhsT_scale=shift_scales[:, a, :].bitcast(U8)[:, P * u : P * (u + 1)],
+                rhs=h_codes[a, hf][:, j0:j1].bitcast(FP8X4),
+                rhs_scale=h_scales[a, hf][:, j0:j1],
+                start=(a == 0),
+                stop=(a == 1),
+            )
+
+        def scenarios_narrow(ch):
+            hf, j0 = divmod(ch * CH, HALF)
+            bank = psum.tile([P, N // P, CH], F32, name="narrow")
+            for u in range(N // P):
+                for a in range(2):
+                    scenario_pass(bank[:, u, :], u, a, hf, j0, j0 + CH)
+            result = kept([P, N // P, CH], F32, f"result_narrow{ch}")
+            if ch == NCH - 1:
+                nc.vector.tensor_tensor(
+                    out=result[:], in0=bank[:], in1=rate[:].unsqueeze(2).to_broadcast([P, N // P, CH]), op=MULT
+                )
+            else:
+                for u in range(N // P):
+                    nc.scalar.activation(out=result[:, u, :], in_=bank[:, u, :], func=COPY, scale=rate[:, u : u + 1])
+            nc.sync.dma_start(out=out[:, ch * CH : (ch + 1) * CH].rearrange("(u p) j -> p u j", p=P), in_=result[:])
+
+        halves = (0, KP // 2, KP)
+        curve_w, curve_s = curve_words[:].bitcast(U32), curve_scales[:].bitcast(U8)
+        gather(v_words, curve_w, idx, 0, HALF)
+        gather(v_words, curve_w, idx, HALF, S)
+        gather(v_scales, curve_s, idx, 0, HALF)
+        round_piece("w1_0", nc.scalar.copy, halves)
+        quantize_piece("w1_0")
+        gather(v_scales, curve_s, idx, HALF, S)
+        discount(0, 0)
+        discount(0, 1)
+        gather(v2_words[0], cash_words[0][:].bitcast(U32), idx2, 0, S)
+        round_piece("w2_00", nc.vector.tensor_copy)
+        gather(v2_scales, cash_scales[:].bitcast(U8), idx2, 0, S)
+        quantize_piece("w2_00")
+        round_piece("w1_1", nc.scalar.copy)
+        round_piece("w2_01", nc.vector.tensor_copy)
+        quantize_piece("w1_1")
+        quantize_piece("w2_01")
+        discount(1, 0)
+        discount(1, 1)
+        for hf in range(2):
+            gather(v2_words[1], cash_words[1][:].bitcast(U32), idx2, hf * HALF, (hf + 1) * HALF)
+        round_piece("w2_10", nc.scalar.copy)
+        round_piece("w2_11", nc.scalar.copy, halves)
+
+        for ch in range(NCH):
+            present_value(0, ch)
+            if ch > 0:
+                quantize_value(0, ch - 1)
+            if ch == 3:
+                quantize_piece("w2_10")
+            if ch == 6:
+                quantize_piece("w2_11")
+        wide = [psum.tile([P, HALF], F32, name="wide") for u in range(N // P)]
+        for u in range(N // P):
+            scenario_pass(wide[u][:], u, 0, 0, 0, HALF)
+        for ch in range(NCH):
+            present_value(1, ch)
+            if ch == 0:
+                quantize_value(0, NCH - 1)
+            else:
+                quantize_value(1, ch - 1)
+            if ch == NCH // 2:
+                for u in range(N // P):
+                    scenario_pass(wide[u][:], u, 1, 0, 0, HALF)
+                    result = kept([P, HALF], F32, f"result_wide{u}")
+                    nc.scalar.activation(out=result[:], in_=wide[u][:], func=COPY, scale=rate[:, u : u + 1])
+                    nc.sync.dma_start(out=out[u * P : (u + 1) * P, 0:HALF], in_=result[:])
+            if ch > NCH // 2:
+                scenarios_narrow(ch - 1)
+        quantize_value(1, NCH - 1)
+        scenarios_narrow(NCH - 1)

@@ -81,33 +81,31 @@ def tile_list_scenario_cashflow_values_kernel(
         def load_words(tile, words, c0=0, c1=None):
             nc.sync.dma_start(out=tile[:, c0:c1], in_=words.rearrange("p t i -> p (t i)").bitcast(I32)[:, c0:c1])
 
+        load_words(curve_words, tab_words[0])
         nc.sync.dma_start(idx[:], offs)
-        nc.sync.dma_start(idx2[:], offs2)
-        nc.sync.dma_start(out=bias[:], in_=b1.rearrange("(a p t) -> p a t", a=2, t=PACK))
-        with nc.allow_non_contiguous_dma(reason="one rate to a partition and output tile"):
-            nc.sync.dma_start(out=rate[:], in_=fx.rearrange("(u p) -> p u", p=P))
         for q in range(4):
             nc.sync.dma_start(out=curve_scales[32 * q : 32 * q + 4, :], in_=tab_scales[0, 4 * q : 4 * q + 4, :].bitcast(I32))
-        load_words(curve_words, tab_words[0], 0, T // 2)
-        load_words(curve_words, tab_words[0], T // 2, T)
-        load_piece("w1_0", 0, KP // 2)
-        load_piece("w1_0", KP // 2, KP)
-        load_words(cash_words[0], tab2_words[0])
+        load_piece("w1_0")
+        nc.sync.dma_start(out=bias[:], in_=b1.rearrange("(a p t) -> p a t", a=2, t=PACK))
+        nc.sync.dma_start(idx2[:], offs2)
         load_cash_scales(0)
-        load_piece("w2_00")
+        load_words(cash_words[0], tab2_words[0])
         load_cash_scales(1)
+        load_piece("w2_00")
         load_piece("w1_1")
+        for q in range(4):
+            nc.sync.dma_start(
+                out=shift_scales[32 * q : 32 * q + 4, :, :],
+                in_=w4_scales[:, 4 * q : 4 * q + 4, :].bitcast(I32).rearrange("a r n -> r a n"),
+            )
         load_piece("w2_01")
         load_words(cash_words[1], tab2_words[1])
         load_piece("w2_10")
         load_piece("w2_11", 0, KP // 2)
         load_piece("w2_11", KP // 2, KP)
         nc.sync.dma_start(out=shift_words[:], in_=w4_words.bitcast(I32).rearrange("a p n -> p a n"))
-        for q in range(4):
-            nc.sync.dma_start(
-                out=shift_scales[32 * q : 32 * q + 4, :, :],
-                in_=w4_scales[:, 4 * q : 4 * q + 4, :].bitcast(I32).rearrange("a r n -> r a n"),
-            )
+        with nc.allow_non_contiguous_dma(reason="one rate to a partition and output tile"):
+            nc.sync.dma_start(out=rate[:], in_=fx.rearrange("(u p) -> p u", p=P))
 
         def gather(dst, window, lst, j0, j1):
             nc.vector.tensor_copy(dst[:, j0:j1], window.indirect(lst[:, j0 // 16 : j1 // 16]))
@@ -115,7 +113,10 @@ def tile_list_scenario_cashflow_values_kernel(
         rounded = {}
 
         def round_piece(name, copy, cuts=(0, KP)):
-            grouped = ring.tile([P, PACK, P, PACK], BF16, name="grouped", align_bytes=64)
+            if name == "w2_11":
+                grouped = kept([P, PACK, P, PACK], BF16, "last_rounded")
+            else:
+                grouped = ring.tile([P, PACK, P, PACK], BF16, name="grouped", align_bytes=64)
             for c0, c1 in zip(cuts[:-1], cuts[1:]):
                 copy(
                     out=grouped[:, :, c0 // PACK : c1 // PACK, :].rearrange("p t m j -> p m j t"),
@@ -146,7 +147,11 @@ def tile_list_scenario_cashflow_values_kernel(
                 )
                 nc.scalar.activation(out=disc[a, hf][:, t, :], in_=bank[:], func=EXP, bias=bias[:, a, t : t + 1])
 
+        runs = {0: [(0, 4), (4, 6), (6, 8)], 1: [(0, 4), (4, 5), (5, 6), (6, 7), (7, 8)]}
         values = {}
+
+        def run_of(a, ch):
+            return [run for run in runs[a] if run[0] <= ch < run[1]][0]
 
         def present_value(a, ch):
             cols = slice(ch * CH, (ch + 1) * CH)
@@ -164,21 +169,26 @@ def tile_list_scenario_cashflow_values_kernel(
                         stop=(g == 1),
                     )
             hf, j0 = divmod(ch * CH, HALF)
-            value = ring.tile([P, CH, PACK], BF16, name="value", align_bytes=64)
+            run = run_of(a, ch)
+            if ch == run[0]:
+                name = "last_rounded" if (a, run) == (0, (6, 8)) else f"values{a}{ch}"
+                values[a, run] = kept([P, (run[1] - run[0]) * CH, PACK], BF16, name)
+            i0 = (ch - run[0]) * CH
             nc.vector.tensor_tensor(
-                out=value[:].rearrange("p (c i) t -> p c t i", i=4),
+                out=values[a, run][:, i0 : i0 + CH, :].rearrange("p (c i) t -> p c t i", i=4),
                 in0=bank[:].rearrange("p t (c i) -> p c t i", i=4),
                 in1=disc[a, hf][:, :, j0 : j0 + CH].rearrange("p t (c i) -> p c t i", i=4),
                 op=MULT,
             )
-            values[a, ch] = value
 
         def quantize_value(a, ch):
-            hf, j0 = divmod(ch * CH, HALF)
+            run = run_of(a, ch)
+            hf, j0 = divmod(run[0] * CH, HALF)
+            j1 = j0 + (run[1] - run[0]) * CH
             nc.vector.quantize_mx(
-                out=h_codes[a, hf][:, j0 : j0 + CH].bitcast(FP8X4),
-                scales=h_scales[a, hf][:, j0 : j0 + CH],
-                in_=values[a, ch][:].rearrange("p j t -> p (j t)"),
+                out=h_codes[a, hf][:, j0:j1].bitcast(FP8X4),
+                scales=h_scales[a, hf][:, j0:j1],
+                in_=values[a, run][:].rearrange("p j t -> p (j t)"),
             )
 
         def scenario_pass(dst, u, a, hf, j0, j1):
@@ -213,21 +223,21 @@ def tile_list_scenario_cashflow_values_kernel(
         gather(v_words, curve_w, idx, 0, HALF)
         gather(v_words, curve_w, idx, HALF, S)
         gather(v_scales, curve_s, idx, 0, HALF)
-        round_piece("w1_0", nc.scalar.copy, halves)
+        round_piece("w1_0", nc.scalar.copy)
         quantize_piece("w1_0")
         gather(v_scales, curve_s, idx, HALF, S)
         discount(0, 0)
         discount(0, 1)
         gather(v2_words[0], cash_words[0][:].bitcast(U32), idx2, 0, S)
-        round_piece("w2_00", nc.vector.tensor_copy)
         gather(v2_scales, cash_scales[:].bitcast(U8), idx2, 0, S)
+        round_piece("w2_00", nc.vector.tensor_copy)
         quantize_piece("w2_00")
         round_piece("w1_1", nc.scalar.copy)
-        round_piece("w2_01", nc.vector.tensor_copy)
         quantize_piece("w1_1")
-        quantize_piece("w2_01")
         discount(1, 0)
         discount(1, 1)
+        round_piece("w2_01", nc.vector.tensor_copy)
+        quantize_piece("w2_01")
         for hf in range(2):
             gather(v2_words[1], cash_words[1][:].bitcast(U32), idx2, hf * HALF, (hf + 1) * HALF)
         round_piece("w2_10", nc.scalar.copy)
@@ -235,28 +245,30 @@ def tile_list_scenario_cashflow_values_kernel(
 
         for ch in range(NCH):
             present_value(0, ch)
-            if ch > 0:
-                quantize_value(0, ch - 1)
-            if ch == 3:
+            if ch == 1:
                 quantize_piece("w2_10")
-            if ch == 6:
+            if ch == 3:
                 quantize_piece("w2_11")
+            if ch == 4:
+                quantize_value(0, 0)
+            if ch == 6:
+                quantize_value(0, 4)
         wide = [psum.tile([P, HALF], F32, name="wide") for u in range(N // P)]
         for u in range(N // P):
             scenario_pass(wide[u][:], u, 0, 0, 0, HALF)
         for ch in range(NCH):
             present_value(1, ch)
             if ch == 0:
-                quantize_value(0, NCH - 1)
-            else:
-                quantize_value(1, ch - 1)
+                quantize_value(0, 6)
             if ch == NCH // 2:
+                quantize_value(1, 0)
                 for u in range(N // P):
                     scenario_pass(wide[u][:], u, 1, 0, 0, HALF)
                     result = kept([P, HALF], F32, f"result_wide{u}")
                     nc.scalar.activation(out=result[:], in_=wide[u][:], func=COPY, scale=rate[:, u : u + 1])
                     nc.sync.dma_start(out=out[u * P : (u + 1) * P, 0:HALF], in_=result[:])
             if ch > NCH // 2:
+                quantize_value(1, ch - 1)
                 scenarios_narrow(ch - 1)
         quantize_value(1, NCH - 1)
         scenarios_narrow(NCH - 1)

@@ -68,10 +68,10 @@ def tile_list_scenario_cashflow_values_kernel(
         nc.vector.memset(cash_scales[:], 0)
         nc.vector.memset(shift_scales[:], 0)
 
-        def load_cash_scales(g):
-            for q in range(4):
-                p0 = 32 * q + 4 + 4 * g
-                nc.sync.dma_start(out=cash_scales[p0 : p0 + 4, :], in_=tab2_scales[g, 4 * q : 4 * q + 4, :].bitcast(I32))
+        def load_cash_scales(rows):
+            for r in rows:
+                for g in range(2):
+                    nc.sync.dma_start(out=cash_scales[4 + 4 * g + r : P : 32, :], in_=tab2_scales[g].bitcast(I32)[r:16:4, :])
 
         def load_piece(name, c0=0, c1=KP):
             w, g, a = pieces[name]
@@ -83,20 +83,20 @@ def tile_list_scenario_cashflow_values_kernel(
 
         load_words(curve_words, tab_words[0])
         nc.sync.dma_start(idx[:], offs)
-        for q in range(4):
-            nc.sync.dma_start(out=curve_scales[32 * q : 32 * q + 4, :], in_=tab_scales[0, 4 * q : 4 * q + 4, :].bitcast(I32))
+        for r in range(4):
+            nc.sync.dma_start(out=curve_scales[r:P:32, :], in_=tab_scales[0].bitcast(I32)[r:16:4, :])
         load_piece("w1_0")
         nc.sync.dma_start(out=bias[:], in_=b1.rearrange("(a p t) -> p a t", a=2, t=PACK))
         nc.sync.dma_start(idx2[:], offs2)
-        load_cash_scales(0)
+        load_cash_scales((0, 1))
         load_words(cash_words[0], tab2_words[0])
-        load_cash_scales(1)
+        load_cash_scales((2, 3))
         load_piece("w2_00")
         load_piece("w1_1")
-        for q in range(4):
+        for r in range(4):
             nc.sync.dma_start(
-                out=shift_scales[32 * q : 32 * q + 4, :, :],
-                in_=w4_scales[:, 4 * q : 4 * q + 4, :].bitcast(I32).rearrange("a r n -> r a n"),
+                out=shift_scales[r:P:32, :, :],
+                in_=w4_scales.bitcast(I32)[:, r:16:4, :].rearrange("a q n -> q a n"),
             )
         load_piece("w2_01")
         load_words(cash_words[1], tab2_words[1])

@@ -51,7 +51,8 @@ def tile_list_scenario_cashflow_values_kernel(
         v_words = kept([P, S], U32, "v_words")
         v_scales = kept([P, S], U8, "v_scales")
         v2_words = [kept([P, S], U32, f"v2_words{a}") for a in range(2)]
-        v2_scales = kept([P, S], U8, "v2_scales")
+        v2_rows = kept([P, S], U8, "v2_rows")
+        v2_scales = kept([P, S // 4], I32, "v2_scales")
 
         pieces = {
             "w1_0": (w1, 0, 0), "w1_1": (w1, 0, 1),
@@ -67,11 +68,21 @@ def tile_list_scenario_cashflow_values_kernel(
         nc.gpsimd.memset(curve_scales[:], 0)
         nc.vector.memset(cash_scales[:], 0)
         nc.vector.memset(shift_scales[:], 0)
+        nc.vector.memset(v2_scales[:], 0)
 
-        def load_cash_scales(rows):
+        def place_cash_scales(rows):
             for r in rows:
                 for g in range(2):
-                    nc.sync.dma_start(out=cash_scales[4 + 4 * g + r : P : 32, :], in_=tab2_scales[g].bitcast(I32)[r:16:4, :])
+                    nc.sync.dma_start(
+                        out=v2_scales[4 + 4 * g + r : P : 32, :],
+                        in_=v2_rows[:].bitcast(I32)[64 * g + 4 * r : 64 * (g + 1) : 16, :],
+                    )
+
+        def load_shift_scales(r):
+            nc.sync.dma_start(
+                out=shift_scales[r:P:32, :, :],
+                in_=w4_scales.bitcast(I32)[:, r:16:4, :].rearrange("a q n -> q a n"),
+            )
 
         def load_piece(name, c0=0, c1=KP):
             w, g, a = pieces[name]
@@ -88,48 +99,39 @@ def tile_list_scenario_cashflow_values_kernel(
         load_piece("w1_0")
         nc.sync.dma_start(out=bias[:], in_=b1.rearrange("(a p t) -> p a t", a=2, t=PACK))
         nc.sync.dma_start(idx2[:], offs2)
-        load_cash_scales((0, 1))
+        for r in range(3):
+            load_shift_scales(r)
+        nc.sync.dma_start(out=cash_scales[0:P:4, :], in_=tab2_scales.bitcast(I32).rearrange("a q t -> (a q) t"))
         load_words(cash_words[0], tab2_words[0])
-        load_cash_scales((2, 3))
+        load_shift_scales(3)
         load_piece("w2_00")
         load_piece("w1_1")
-        for r in range(4):
-            nc.sync.dma_start(
-                out=shift_scales[r:P:32, :, :],
-                in_=w4_scales.bitcast(I32)[:, r:16:4, :].rearrange("a q n -> q a n"),
-            )
-        load_piece("w2_01")
-        load_words(cash_words[1], tab2_words[1])
-        load_piece("w2_10")
-        load_piece("w2_11", 0, KP // 2)
-        load_piece("w2_11", KP // 2, KP)
-        nc.sync.dma_start(out=shift_words[:], in_=w4_words.bitcast(I32).rearrange("a p n -> p a n"))
-        with nc.allow_non_contiguous_dma(reason="one rate to a partition and output tile"):
-            nc.sync.dma_start(out=rate[:], in_=fx.rearrange("(u p) -> p u", p=P))
 
         def gather(dst, window, lst, j0, j1):
             nc.vector.tensor_copy(dst[:, j0:j1], window.indirect(lst[:, j0 // 16 : j1 // 16]))
 
         rounded = {}
 
-        def round_piece(name, copy, cuts=(0, KP)):
+        def round_piece(name, *shares):
             if name == "w2_11":
                 grouped = kept([P, PACK, P, PACK], BF16, "last_rounded")
             else:
                 grouped = ring.tile([P, PACK, P, PACK], BF16, name="grouped", align_bytes=64)
-            for c0, c1 in zip(cuts[:-1], cuts[1:]):
+            for copy, c0, c1 in shares:
                 copy(
                     out=grouped[:, :, c0 // PACK : c1 // PACK, :].rearrange("p t m j -> p m j t"),
                     in_=raw[name][:, :, c0:c1].rearrange("p j (m t) -> p m j t", t=PACK),
                 )
             rounded[name] = grouped
 
-        def quantize_piece(name):
-            nc.vector.quantize_mx(
-                out=w_codes[name][:].bitcast(FP8X4),
-                scales=w_scales[name][:],
-                in_=rounded[name][:].rearrange("p t m j -> p (t m j)"),
-            )
+        def quantize_piece(name, calls=1):
+            for i in range(calls):
+                t0, t1 = i * PACK // calls, (i + 1) * PACK // calls
+                nc.vector.quantize_mx(
+                    out=w_codes[name][:, t0 * P : t1 * P].bitcast(FP8X4),
+                    scales=w_scales[name][:, t0 * P : t1 * P],
+                    in_=rounded[name][:, t0:t1, :, :].rearrange("p t m j -> p (t m j)"),
+                )
 
         def discount(a, hf):
             name = f"w1_{a}"
@@ -147,7 +149,7 @@ def tile_list_scenario_cashflow_values_kernel(
                 )
                 nc.scalar.activation(out=disc[a, hf][:, t, :], in_=bank[:], func=EXP, bias=bias[:, a, t : t + 1])
 
-        runs = {0: [(0, 4), (4, 6), (6, 8)], 1: [(0, 4), (4, 5), (5, 6), (6, 7), (7, 8)]}
+        runs = {0: [(0, 4), (4, 6), (6, 8)], 1: [(0, 2), (2, 4), (4, 5), (5, 6), (6, 7), (7, 8)]}
         values = {}
 
         def run_of(a, ch):
@@ -164,7 +166,7 @@ def tile_list_scenario_cashflow_values_kernel(
                         lhsT=w_codes[name][:, t * P : (t + 1) * P].bitcast(FP8X4),
                         lhsT_scale=w_scales[name][:, t * P : (t + 1) * P],
                         rhs=v2_words[g][:, cols].bitcast(FP8X4),
-                        rhs_scale=v2_scales[4 + 4 * g : P, cols],
+                        rhs_scale=v2_scales[:].bitcast(U8)[4 + 4 * g : P, cols],
                         start=(g == 0),
                         stop=(g == 1),
                     )
@@ -181,14 +183,15 @@ def tile_list_scenario_cashflow_values_kernel(
                 op=MULT,
             )
 
-        def quantize_value(a, ch):
+        def quantize_value(a, ch, count):
             run = run_of(a, ch)
-            hf, j0 = divmod(run[0] * CH, HALF)
-            j1 = j0 + (run[1] - run[0]) * CH
+            hf, j0 = divmod(ch * CH, HALF)
+            j1 = j0 + count * CH
+            i0 = (ch - run[0]) * CH
             nc.vector.quantize_mx(
                 out=h_codes[a, hf][:, j0:j1].bitcast(FP8X4),
                 scales=h_scales[a, hf][:, j0:j1],
-                in_=values[a, run][:].rearrange("p j t -> p (j t)"),
+                in_=values[a, run][:, i0 : i0 + count * CH, :].rearrange("p j t -> p (j t)"),
             )
 
         def scenario_pass(dst, u, a, hf, j0, j1):
@@ -202,73 +205,104 @@ def tile_list_scenario_cashflow_values_kernel(
                 stop=(a == 1),
             )
 
-        def scenarios_narrow(ch):
+        def scenarios_narrow(ch, result, u0=0, u1=N // P, on_vector=False):
             hf, j0 = divmod(ch * CH, HALF)
-            bank = psum.tile([P, N // P, CH], F32, name="narrow")
-            for u in range(N // P):
+            bank = psum.tile([P, u1 - u0, CH], F32, name="narrow")
+            for u in range(u0, u1):
                 for a in range(2):
-                    scenario_pass(bank[:, u, :], u, a, hf, j0, j0 + CH)
-            result = kept([P, N // P, CH], F32, f"result_narrow{ch}")
-            if ch == NCH - 1:
+                    scenario_pass(bank[:, u - u0, :], u, a, hf, j0, j0 + CH)
+            if on_vector:
                 nc.vector.tensor_tensor(
-                    out=result[:], in0=bank[:], in1=rate[:].unsqueeze(2).to_broadcast([P, N // P, CH]), op=MULT
+                    out=result, in0=bank[:], in1=rate[:, u0:u1].unsqueeze(2).to_broadcast([P, u1 - u0, CH]), op=MULT
                 )
             else:
-                for u in range(N // P):
-                    nc.scalar.activation(out=result[:, u, :], in_=bank[:, u, :], func=COPY, scale=rate[:, u : u + 1])
-            nc.sync.dma_start(out=out[:, ch * CH : (ch + 1) * CH].rearrange("(u p) j -> p u j", p=P), in_=result[:])
+                for u in range(u0, u1):
+                    nc.scalar.activation(
+                        out=result[:, u - u0, :], in_=bank[:, u - u0, :], func=COPY, scale=rate[:, u : u + 1]
+                    )
 
-        halves = (0, KP // 2, KP)
+        def store(result, u0, u1, j0, j1):
+            nc.sync.dma_start(out=out[u0 * P : u1 * P, j0:j1].rearrange("(u p) j -> p u j", p=P), in_=result)
+
+        on_scalar, on_vector = nc.scalar.copy, nc.vector.tensor_copy
         curve_w, curve_s = curve_words[:].bitcast(U32), curve_scales[:].bitcast(U8)
         gather(v_words, curve_w, idx, 0, HALF)
         gather(v_words, curve_w, idx, HALF, S)
         gather(v_scales, curve_s, idx, 0, HALF)
-        round_piece("w1_0", nc.scalar.copy)
+        round_piece("w1_0", (on_scalar, 0, KP))
         quantize_piece("w1_0")
         gather(v_scales, curve_s, idx, HALF, S)
         discount(0, 0)
         discount(0, 1)
+        gather(v2_rows, cash_scales[:].bitcast(U8), idx2, 0, S)
+
+        place_cash_scales((0, 1))
+        load_piece("w2_01")
+        load_words(cash_words[1], tab2_words[1])
+        place_cash_scales((2, 3))
+        load_piece("w2_10")
+        load_piece("w2_11", 0, KP // 2)
+        load_piece("w2_11", KP // 2, KP)
+        nc.sync.dma_start(out=shift_words[:], in_=w4_words.bitcast(I32).rearrange("a p n -> p a n"))
+        with nc.allow_non_contiguous_dma(reason="one rate to a partition and output tile"):
+            nc.sync.dma_start(out=rate[:], in_=fx.rearrange("(u p) -> p u", p=P))
+
         gather(v2_words[0], cash_words[0][:].bitcast(U32), idx2, 0, S)
-        gather(v2_scales, cash_scales[:].bitcast(U8), idx2, 0, S)
-        round_piece("w2_00", nc.vector.tensor_copy)
+        round_piece("w2_00", (on_vector, 0, KP))
         quantize_piece("w2_00")
-        round_piece("w1_1", nc.scalar.copy)
+        round_piece("w1_1", (on_scalar, 0, KP))
         quantize_piece("w1_1")
         discount(1, 0)
         discount(1, 1)
-        round_piece("w2_01", nc.vector.tensor_copy)
+        round_piece("w2_01", (on_vector, 0, KP))
         quantize_piece("w2_01")
         for hf in range(2):
             gather(v2_words[1], cash_words[1][:].bitcast(U32), idx2, hf * HALF, (hf + 1) * HALF)
-        round_piece("w2_10", nc.scalar.copy)
-        round_piece("w2_11", nc.scalar.copy, halves)
+        round_piece("w2_10", (on_scalar, 0, KP))
+        round_piece("w2_11", (on_scalar, 0, KP // 2), (on_scalar, KP // 2, KP))
 
-        for ch in range(NCH):
+        for ch in range(NCH - 1):
             present_value(0, ch)
             if ch == 1:
                 quantize_piece("w2_10")
             if ch == 3:
-                quantize_piece("w2_11")
+                quantize_piece("w2_11", 2)
             if ch == 4:
-                quantize_value(0, 0)
-            if ch == 6:
-                quantize_value(0, 4)
+                quantize_value(0, 0, 4)
+        quantize_value(0, 4, 2)
         wide = [psum.tile([P, HALF], F32, name="wide") for u in range(N // P)]
         for u in range(N // P):
             scenario_pass(wide[u][:], u, 0, 0, 0, HALF)
-        for ch in range(NCH):
-            present_value(1, ch)
-            if ch == 0:
-                quantize_value(0, 6)
-            if ch == NCH // 2:
-                quantize_value(1, 0)
-                for u in range(N // P):
-                    scenario_pass(wide[u][:], u, 1, 0, 0, HALF)
-                    result = kept([P, HALF], F32, f"result_wide{u}")
-                    nc.scalar.activation(out=result[:], in_=wide[u][:], func=COPY, scale=rate[:, u : u + 1])
-                    nc.sync.dma_start(out=out[u * P : (u + 1) * P, 0:HALF], in_=result[:])
-            if ch > NCH // 2:
-                quantize_value(1, ch - 1)
-                scenarios_narrow(ch - 1)
-        quantize_value(1, NCH - 1)
-        scenarios_narrow(NCH - 1)
+        present_value(1, 0)
+        present_value(1, 1)
+        present_value(1, 2)
+        quantize_value(1, 0, 2)
+        present_value(1, 3)
+        quantize_value(0, 6, 1)
+        quantize_value(1, 2, 2)
+        present_value(0, 7)
+        present_value(1, 4)
+        quantize_value(0, 7, 1)
+        for u in range(N // P):
+            scenario_pass(wide[u][:], u, 1, 0, 0, HALF)
+            result = kept([P, 1, HALF], F32, f"result_wide{u}")
+            nc.scalar.activation(out=result[:, 0, :], in_=wide[u][:], func=COPY, scale=rate[:, u : u + 1])
+            store(result[:], u, u + 1, 0, HALF)
+        present_value(1, 5)
+        quantize_value(1, 4, 1)
+        present_value(1, 6)
+        quantize_value(1, 5, 1)
+        pair = kept([P, N // P, 2 * CH], F32, "result_pair")
+        scenarios_narrow(4, pair[:, :, 0:CH])
+        present_value(1, 7)
+        quantize_value(1, 6, 1)
+        scenarios_narrow(5, pair[:, :, CH : 2 * CH])
+        store(pair[:], 0, N // P, 4 * CH, 6 * CH)
+        quantize_value(1, 7, 1)
+        single = kept([P, N // P, CH], F32, "result_single")
+        scenarios_narrow(6, single[:])
+        store(single[:], 0, N // P, 6 * CH, 7 * CH)
+        for u0 in (0, 2):
+            last = kept([P, 2, CH], F32, f"result_last{u0}")
+            scenarios_narrow(7, last[:], u0, u0 + 2, on_vector=(u0 == 0))
+            store(last[:], u0, u0 + 2, 7 * CH, 8 * CH)

@@ -18,12 +18,24 @@ COPY = mybir.ActivationFunctionType.Copy
 MULT = mybir.AluOpType.mult
 
 P = 128
+QUADRANT = 32
+SCALE_ROWS = 4
+BLOCKS = 16
 PACK = 4
 KP = P * PACK
+I32_BYTES = 4
+LIST_GROUP = 16
 HALF = 512
 CH = 128
-NCH = S // CH
-LIST_COLS = S // 16
+LINE = 4
+OUT_TILES = N // P
+DISCOUNT_BANKS = 2
+
+W2_PIECES = {"w2_00": (0, 0), "w2_01": (1, 0), "w2_10": (0, 1), "w2_11": (1, 1)}
+PIECES = ["w1_0", "w1_1", *W2_PIECES]
+
+RUNS = {0: [(0, 4), (4, 6), (6, 7), (7, 8)], 1: [(0, 2), (2, 4), (4, 5), (5, 6), (6, 7), (7, 8)]}
+RUN_TILE = {(0, 6): "last_rounded", (0, 7): "values10"}
 
 
 def tile_list_scenario_cashflow_values_kernel(
@@ -38,86 +50,62 @@ def tile_list_scenario_cashflow_values_kernel(
         def kept(shape, dtype, name):
             return keep.tile(shape, dtype, name=name, align_bytes=64)
 
-        idx = kept([P, LIST_COLS], U16, "idx")
-        idx2 = kept([P, LIST_COLS], U16, "idx2")
+        idx = kept([P, S // LIST_GROUP], U16, "idx")
+        idx2 = kept([P, S // LIST_GROUP], U16, "idx2")
         curve_words = kept([P, T], I32, "curve_words")
-        curve_scales = kept([P, T // 4], I32, "curve_scales")
-        cash_words = [kept([P, T2], I32, f"cash_words{a}") for a in range(2)]
-        cash_scales = kept([P, T2 // 4], I32, "cash_scales")
-        shift_words = kept([P, 2, 2 * N // 4], I32, "shift_words")
-        shift_scales = kept([P, 2, N // 4], I32, "shift_scales")
+        curve_scales = kept([P, T // I32_BYTES], I32, "curve_scales")
+        cash_words = [kept([P, T2], I32, f"cash_words{g}") for g in range(2)]
+        cash_scales = kept([P, T2 // I32_BYTES], I32, "cash_scales")
+        shift_words = kept([P, 2, 2 * N // I32_BYTES], I32, "shift_words")
+        shift_scales = kept([P, 2, N // I32_BYTES], I32, "shift_scales")
         bias = kept([P, 2, PACK], F32, "bias")
-        rate = kept([P, N // P], F32, "rate")
+        rate = kept([P, OUT_TILES], F32, "rate")
         v_words = kept([P, S], U32, "v_words")
         v_scales = kept([P, S], U8, "v_scales")
-        v2_words = [kept([P, S], U32, f"v2_words{a}") for a in range(2)]
+        v2_words = [kept([P, S], U32, f"v2_words{g}") for g in range(2)]
         v2_rows = kept([P, S], U8, "v2_rows")
-        v2_scales = kept([P, S // 4], I32, "v2_scales")
+        v2_scales = kept([P, S // I32_BYTES], I32, "v2_scales")
 
-        pieces = {
-            "w1_0": (w1, 0, 0), "w1_1": (w1, 0, 1),
-            "w2_00": (w2, 0, 0), "w2_01": (w2, 1, 0), "w2_10": (w2, 0, 1), "w2_11": (w2, 1, 1),
-        }
-        raw = {name: kept([P, PACK, KP], F32, "raw_" + name) for name in pieces}
-        w_codes = {name: kept([P, KP], U32, "codes_" + name) for name in pieces}
-        w_scales = {name: kept([P, KP], U8, "scales_" + name) for name in pieces}
+        raw_w1 = kept([P, PACK, H], F32, "raw_w1")
+        raw = {name: kept([P, PACK, KP], F32, "raw_" + name) for name in W2_PIECES}
+        raw["w1_0"], raw["w1_1"] = raw_w1[:, :, 0:KP], raw_w1[:, :, KP:H]
+        w_codes = {name: kept([P, KP], U32, "codes_" + name) for name in PIECES if name != "w1_1"}
+        w_scales = {name: kept([P, KP], U8, "scales_" + name) for name in PIECES}
         disc = {(a, hf): kept([P, PACK, HALF], F32, f"disc{a}{hf}") for a in range(2) for hf in range(2)}
-        h_codes = {(a, hf): kept([P, HALF], U32, f"h_codes{a}{hf}") for a in range(2) for hf in range(2)}
+        h_codes = {(a, hf): kept([P, HALF], U32, f"h_codes{a}{hf}") for a, hf in ((0, 0), (1, 0), (1, 1))}
         h_scales = {(a, hf): kept([P, HALF], U8, f"h_scales{a}{hf}") for a in range(2) for hf in range(2)}
+        rounded, values = {}, {}
 
         nc.gpsimd.memset(curve_scales[:], 0)
         nc.vector.memset(cash_scales[:], 0)
         nc.vector.memset(shift_scales[:], 0)
         nc.vector.memset(v2_scales[:], 0)
 
-        def place_cash_scales(rows):
-            for r in rows:
-                for g in range(2):
-                    nc.sync.dma_start(
-                        out=v2_scales[4 + 4 * g + r : P : 32, :],
-                        in_=v2_rows[:].bitcast(I32)[64 * g + 4 * r : 64 * (g + 1) : 16, :],
-                    )
+        def load_words(tile, words):
+            nc.sync.dma_start(out=tile[:], in_=words.rearrange("p t i -> p (t i)").bitcast(I32))
 
-        def load_shift_scales(r):
-            nc.sync.dma_start(
-                out=shift_scales[r:P:32, :, :],
-                in_=w4_scales.bitcast(I32)[:, r:16:4, :].rearrange("a q n -> q a n"),
-            )
-
-        def load_piece(name, c0=0, c1=KP):
-            w, g, a = pieces[name]
-            src = w[g * KP : (g + 1) * KP, a * KP + c0 : a * KP + c1]
+        def load_w2(name, c0=0, c1=KP):
+            g, a = W2_PIECES[name]
+            src = w2[g * KP : (g + 1) * KP, a * KP + c0 : a * KP + c1]
             nc.sync.dma_start(out=raw[name][:, :, c0:c1], in_=src.rearrange("(p j) c -> p j c", j=PACK))
 
-        def load_words(tile, words, c0=0, c1=None):
-            nc.sync.dma_start(out=tile[:, c0:c1], in_=words.rearrange("p t i -> p (t i)").bitcast(I32)[:, c0:c1])
+        def place_cash_scales(rows):
+            for s in rows:
+                for g in range(2):
+                    nc.sync.dma_start(
+                        out=v2_scales[SCALE_ROWS * (g + 1) + s : P : QUADRANT, :],
+                        in_=v2_rows[:].bitcast(I32)[4 * (BLOCKS * g + s) : 4 * BLOCKS * (g + 1) : 4 * SCALE_ROWS, :],
+                    )
 
-        load_words(curve_words, tab_words[0])
-        nc.sync.dma_start(idx[:], offs)
-        for r in range(4):
-            nc.sync.dma_start(out=curve_scales[r:P:32, :], in_=tab_scales[0].bitcast(I32)[r:16:4, :])
-        load_piece("w1_0")
-        nc.sync.dma_start(out=bias[:], in_=b1.rearrange("(a p t) -> p a t", a=2, t=PACK))
-        nc.sync.dma_start(idx2[:], offs2)
-        for r in range(3):
-            load_shift_scales(r)
-        nc.sync.dma_start(out=cash_scales[0:P:4, :], in_=tab2_scales.bitcast(I32).rearrange("a q t -> (a q) t"))
-        load_words(cash_words[0], tab2_words[0])
-        load_shift_scales(3)
-        load_piece("w2_00")
-        load_piece("w1_1")
+        def gather(dst, window, offsets, j0, j1):
+            nc.vector.tensor_copy(dst[:, j0:j1], window.indirect(offsets[:, j0 // LIST_GROUP : j1 // LIST_GROUP]))
 
-        def gather(dst, window, lst, j0, j1):
-            nc.vector.tensor_copy(dst[:, j0:j1], window.indirect(lst[:, j0 // 16 : j1 // 16]))
-
-        rounded = {}
-
-        def round_piece(name, *shares):
+        def round_piece(name, copy, cuts=(0, KP)):
             if name == "w2_11":
                 grouped = kept([P, PACK, P, PACK], BF16, "last_rounded")
             else:
                 grouped = ring.tile([P, PACK, P, PACK], BF16, name="grouped", align_bytes=64)
-            for copy, c0, c1 in shares:
+            for c0, c1 in zip(cuts[:-1], cuts[1:]):
                 copy(
                     out=grouped[:, :, c0 // PACK : c1 // PACK, :].rearrange("p t m j -> p m j t"),
                     in_=raw[name][:, :, c0:c1].rearrange("p j (m t) -> p m j t", t=PACK),
@@ -137,7 +125,7 @@ def tile_list_scenario_cashflow_values_kernel(
             name = f"w1_{a}"
             cols = slice(hf * HALF, (hf + 1) * HALF)
             for t in range(PACK):
-                bank = psum.tile([P, HALF], F32, name="wide")
+                bank = psum.tile([P, HALF], F32, name=f"wide{t % DISCOUNT_BANKS}", bufs=1)
                 nc.tensor.matmul_mx(
                     out=bank[:],
                     lhsT=w_codes[name][:, t * P : (t + 1) * P].bitcast(FP8X4),
@@ -148,12 +136,6 @@ def tile_list_scenario_cashflow_values_kernel(
                     stop=True,
                 )
                 nc.scalar.activation(out=disc[a, hf][:, t, :], in_=bank[:], func=EXP, bias=bias[:, a, t : t + 1])
-
-        runs = {0: [(0, 4), (4, 6), (6, 8)], 1: [(0, 2), (2, 4), (4, 5), (5, 6), (6, 7), (7, 8)]}
-        values = {}
-
-        def run_of(a, ch):
-            return [run for run in runs[a] if run[0] <= ch < run[1]][0]
 
         def present_value(a, ch):
             cols = slice(ch * CH, (ch + 1) * CH)
@@ -166,32 +148,30 @@ def tile_list_scenario_cashflow_values_kernel(
                         lhsT=w_codes[name][:, t * P : (t + 1) * P].bitcast(FP8X4),
                         lhsT_scale=w_scales[name][:, t * P : (t + 1) * P],
                         rhs=v2_words[g][:, cols].bitcast(FP8X4),
-                        rhs_scale=v2_scales[:].bitcast(U8)[4 + 4 * g : P, cols],
+                        rhs_scale=v2_scales[:].bitcast(U8)[SCALE_ROWS * (g + 1) : P, cols],
                         start=(g == 0),
                         stop=(g == 1),
                     )
             hf, j0 = divmod(ch * CH, HALF)
-            run = run_of(a, ch)
-            if ch == run[0]:
-                name = "last_rounded" if (a, run) == (0, (6, 8)) else f"values{a}{ch}"
-                values[a, run] = kept([P, (run[1] - run[0]) * CH, PACK], BF16, name)
-            i0 = (ch - run[0]) * CH
+            first, end = [run for run in RUNS[a] if run[0] <= ch < run[1]][0]
+            if ch == first:
+                name = RUN_TILE.get((a, first), f"values{a}{first}")
+                values[a, first] = kept([P, (end - first) * CH, PACK], BF16, name)
+            i0 = (ch - first) * CH
             nc.vector.tensor_tensor(
-                out=values[a, run][:, i0 : i0 + CH, :].rearrange("p (c i) t -> p c t i", i=4),
-                in0=bank[:].rearrange("p t (c i) -> p c t i", i=4),
-                in1=disc[a, hf][:, :, j0 : j0 + CH].rearrange("p t (c i) -> p c t i", i=4),
+                out=values[a, first][:, i0 : i0 + CH, :].rearrange("p (c i) t -> p c t i", i=LINE),
+                in0=bank[:].rearrange("p t (c i) -> p c t i", i=LINE),
+                in1=disc[a, hf][:, :, j0 : j0 + CH].rearrange("p t (c i) -> p c t i", i=LINE),
                 op=MULT,
             )
 
-        def quantize_value(a, ch, count):
-            run = run_of(a, ch)
-            hf, j0 = divmod(ch * CH, HALF)
-            j1 = j0 + count * CH
-            i0 = (ch - run[0]) * CH
+        def quantize_run(a, first):
+            hf, j0 = divmod(first * CH, HALF)
+            j1 = j0 + values[a, first].shape[1]
             nc.vector.quantize_mx(
                 out=h_codes[a, hf][:, j0:j1].bitcast(FP8X4),
                 scales=h_scales[a, hf][:, j0:j1],
-                in_=values[a, run][:, i0 : i0 + count * CH, :].rearrange("p j t -> p (j t)"),
+                in_=values[a, first][:].rearrange("p j t -> p (j t)"),
             )
 
         def scenario_pass(dst, u, a, hf, j0, j1):
@@ -205,104 +185,130 @@ def tile_list_scenario_cashflow_values_kernel(
                 stop=(a == 1),
             )
 
-        def scenarios_narrow(ch, result, u0=0, u1=N // P, on_vector=False):
+        def scenario_bank(ch, u0, u1):
             hf, j0 = divmod(ch * CH, HALF)
             bank = psum.tile([P, u1 - u0, CH], F32, name="narrow")
             for u in range(u0, u1):
                 for a in range(2):
                     scenario_pass(bank[:, u - u0, :], u, a, hf, j0, j0 + CH)
-            if on_vector:
-                nc.vector.tensor_tensor(
-                    out=result, in0=bank[:], in1=rate[:, u0:u1].unsqueeze(2).to_broadcast([P, u1 - u0, CH]), op=MULT
+            return bank
+
+        def apply_rate_on_scalar(result, bank, u0, u1):
+            for u in range(u0, u1):
+                nc.scalar.activation(
+                    out=result[:, u - u0, :], in_=bank[:, u - u0, :], func=COPY, scale=rate[:, u : u + 1]
                 )
-            else:
-                for u in range(u0, u1):
-                    nc.scalar.activation(
-                        out=result[:, u - u0, :], in_=bank[:, u - u0, :], func=COPY, scale=rate[:, u : u + 1]
-                    )
 
         def store(result, u0, u1, j0, j1):
             nc.sync.dma_start(out=out[u0 * P : u1 * P, j0:j1].rearrange("(u p) j -> p u j", p=P), in_=result)
 
-        on_scalar, on_vector = nc.scalar.copy, nc.vector.tensor_copy
-        curve_w, curve_s = curve_words[:].bitcast(U32), curve_scales[:].bitcast(U8)
-        gather(v_words, curve_w, idx, 0, HALF)
-        gather(v_words, curve_w, idx, HALF, S)
-        gather(v_scales, curve_s, idx, 0, HALF)
-        round_piece("w1_0", (on_scalar, 0, KP))
-        quantize_piece("w1_0")
-        gather(v_scales, curve_s, idx, HALF, S)
-        discount(0, 0)
-        discount(0, 1)
+        load_words(curve_words, tab_words[0])
+        nc.sync.dma_start(idx[:], offs)
+        for s in range(SCALE_ROWS):
+            nc.sync.dma_start(
+                out=curve_scales[s:P:QUADRANT, :], in_=tab_scales[0].bitcast(I32)[s:BLOCKS:SCALE_ROWS, :]
+            )
+        nc.sync.dma_start(out=raw_w1[:], in_=w1.rearrange("(p j) c -> p j c", j=PACK))
+        nc.sync.dma_start(idx2[:], offs2)
+        nc.sync.dma_start(out=cash_scales[0:P:4, :], in_=tab2_scales.bitcast(I32).rearrange("g q t -> (g q) t"))
+        nc.sync.dma_start(out=bias[:], in_=b1.rearrange("(a p t) -> p a t", a=2, t=PACK))
+        load_words(cash_words[0], tab2_words[0])
+        for s in range(SCALE_ROWS):
+            nc.sync.dma_start(
+                out=shift_scales[s:P:QUADRANT, :, :],
+                in_=w4_scales.bitcast(I32)[:, s:BLOCKS:SCALE_ROWS, :].rearrange("a q n -> q a n"),
+            )
+        load_w2("w2_00")
+        load_w2("w2_01")
+
+        gather(v_words, curve_words[:].bitcast(U32), idx, 0, S)
+        gather(v_scales, curve_scales[:].bitcast(U8), idx, 0, S)
         gather(v2_rows, cash_scales[:].bitcast(U8), idx2, 0, S)
+        for a in range(2):
+            round_piece(f"w1_{a}", nc.scalar.copy)
+        quantize_piece("w1_0")
+        for hf in range(2):
+            discount(0, hf)
 
         place_cash_scales((0, 1))
-        load_piece("w2_01")
         load_words(cash_words[1], tab2_words[1])
         place_cash_scales((2, 3))
-        load_piece("w2_10")
-        load_piece("w2_11", 0, KP // 2)
-        load_piece("w2_11", KP // 2, KP)
+        load_w2("w2_10")
+        load_w2("w2_11", 0, KP // 2)
+        load_w2("w2_11", KP // 2, KP)
         nc.sync.dma_start(out=shift_words[:], in_=w4_words.bitcast(I32).rearrange("a p n -> p a n"))
         with nc.allow_non_contiguous_dma(reason="one rate to a partition and output tile"):
             nc.sync.dma_start(out=rate[:], in_=fx.rearrange("(u p) -> p u", p=P))
 
         gather(v2_words[0], cash_words[0][:].bitcast(U32), idx2, 0, S)
-        round_piece("w2_00", (on_vector, 0, KP))
-        quantize_piece("w2_00")
-        round_piece("w1_1", (on_scalar, 0, KP))
+        round_piece("w2_00", nc.vector.tensor_copy)
+        w_codes["w1_1"] = kept([P, KP], U32, "raw_w2_00")
         quantize_piece("w1_1")
-        discount(1, 0)
-        discount(1, 1)
-        round_piece("w2_01", (on_vector, 0, KP))
+        quantize_piece("w2_00")
+        for hf in range(2):
+            discount(1, hf)
+        round_piece("w2_01", nc.vector.tensor_copy)
         quantize_piece("w2_01")
         for hf in range(2):
             gather(v2_words[1], cash_words[1][:].bitcast(U32), idx2, hf * HALF, (hf + 1) * HALF)
-        round_piece("w2_10", (on_scalar, 0, KP))
-        round_piece("w2_11", (on_scalar, 0, KP // 2), (on_scalar, KP // 2, KP))
+        round_piece("w2_10", nc.scalar.copy)
+        round_piece("w2_11", nc.scalar.copy, (0, KP // 2, KP))
+        h_codes[0, 1] = kept([P, HALF], U32, "raw_w2_11")
 
-        for ch in range(NCH - 1):
-            present_value(0, ch)
-            if ch == 1:
-                quantize_piece("w2_10")
-            if ch == 3:
-                quantize_piece("w2_11", 2)
-            if ch == 4:
-                quantize_value(0, 0, 4)
-        quantize_value(0, 4, 2)
-        wide = [psum.tile([P, HALF], F32, name="wide") for u in range(N // P)]
-        for u in range(N // P):
+        present_value(0, 0)
+        present_value(0, 1)
+        quantize_piece("w2_10")
+        present_value(0, 2)
+        present_value(0, 3)
+        quantize_piece("w2_11", calls=2)
+        present_value(0, 4)
+        quantize_run(0, 0)
+        present_value(0, 5)
+        present_value(0, 6)
+        quantize_run(0, 4)
+        wide = [psum.tile([P, HALF], F32, name=f"wide{u}", bufs=1) for u in range(OUT_TILES)]
+        for u in range(OUT_TILES):
             scenario_pass(wide[u][:], u, 0, 0, 0, HALF)
+
         present_value(1, 0)
         present_value(1, 1)
         present_value(1, 2)
-        quantize_value(1, 0, 2)
+        quantize_run(1, 0)
         present_value(1, 3)
-        quantize_value(0, 6, 1)
-        quantize_value(1, 2, 2)
+        quantize_run(0, 6)
+        quantize_run(1, 2)
         present_value(0, 7)
         present_value(1, 4)
-        quantize_value(0, 7, 1)
-        for u in range(N // P):
+        quantize_run(0, 7)
+        for u in range(OUT_TILES):
             scenario_pass(wide[u][:], u, 1, 0, 0, HALF)
             result = kept([P, 1, HALF], F32, f"result_wide{u}")
             nc.scalar.activation(out=result[:, 0, :], in_=wide[u][:], func=COPY, scale=rate[:, u : u + 1])
             store(result[:], u, u + 1, 0, HALF)
+
         present_value(1, 5)
-        quantize_value(1, 4, 1)
+        quantize_run(1, 4)
         present_value(1, 6)
-        quantize_value(1, 5, 1)
-        pair = kept([P, N // P, 2 * CH], F32, "result_pair")
-        scenarios_narrow(4, pair[:, :, 0:CH])
+        quantize_run(1, 5)
+        pair = kept([P, OUT_TILES, 2 * CH], F32, "result_pair")
+        apply_rate_on_scalar(pair[:, :, 0:CH], scenario_bank(4, 0, OUT_TILES), 0, OUT_TILES)
         present_value(1, 7)
-        quantize_value(1, 6, 1)
-        scenarios_narrow(5, pair[:, :, CH : 2 * CH])
-        store(pair[:], 0, N // P, 4 * CH, 6 * CH)
-        quantize_value(1, 7, 1)
-        single = kept([P, N // P, CH], F32, "result_single")
-        scenarios_narrow(6, single[:])
-        store(single[:], 0, N // P, 6 * CH, 7 * CH)
-        for u0 in (0, 2):
-            last = kept([P, 2, CH], F32, f"result_last{u0}")
-            scenarios_narrow(7, last[:], u0, u0 + 2, on_vector=(u0 == 0))
-            store(last[:], u0, u0 + 2, 7 * CH, 8 * CH)
+        quantize_run(1, 6)
+        apply_rate_on_scalar(pair[:, :, CH : 2 * CH], scenario_bank(5, 0, OUT_TILES), 0, OUT_TILES)
+        store(pair[:], 0, OUT_TILES, 4 * CH, 6 * CH)
+        quantize_run(1, 7)
+        single = kept([P, OUT_TILES, CH], F32, "result_single")
+        apply_rate_on_scalar(single[:], scenario_bank(6, 0, OUT_TILES), 0, OUT_TILES)
+        store(single[:], 0, OUT_TILES, 6 * CH, 7 * CH)
+        mid = OUT_TILES // 2
+        upper = kept([P, mid, CH], F32, "result_upper")
+        nc.vector.tensor_tensor(
+            out=upper[:],
+            in0=scenario_bank(7, 0, mid)[:],
+            in1=rate[:, 0:mid].unsqueeze(2).to_broadcast([P, mid, CH]),
+            op=MULT,
+        )
+        store(upper[:], 0, mid, 7 * CH, S)
+        lower = kept([P, mid, CH], F32, "result_lower")
+        apply_rate_on_scalar(lower[:], scenario_bank(7, mid, OUT_TILES), mid, OUT_TILES)
+        store(lower[:], mid, OUT_TILES, 7 * CH, S)

@@ -29,7 +29,7 @@ HALF = 512
 CH = 128
 LINE = 4
 OUT_TILES = N // P
-DISCOUNT_BANKS = 2
+DISCOUNT_BANKS = 3
 
 W2_PIECES = {"w2_00": (0, 0), "w2_01": (1, 0), "w2_10": (0, 1), "w2_11": (1, 1)}
 PIECES = ["w1_0", "w1_1", *W2_PIECES]
@@ -58,28 +58,28 @@ def tile_list_scenario_cashflow_values_kernel(
         cash_scales = kept([P, T2 // I32_BYTES], I32, "cash_scales")
         shift_words = kept([P, 2, 2 * N // I32_BYTES], I32, "shift_words")
         shift_scales = kept([P, 2, N // I32_BYTES], I32, "shift_scales")
-        bias = kept([P, 2, PACK], F32, "bias")
+        bias = kept([P, 2, 2 * PACK], F32, "bias")
         rate = kept([P, OUT_TILES], F32, "rate")
         v_words = kept([P, S], U32, "v_words")
-        v_scales = kept([P, S], U8, "v_scales")
         v2_words = [kept([P, S], U32, f"v2_words{g}") for g in range(2)]
-        v2_rows = kept([P, S], U8, "v2_rows")
-        v2_scales = kept([P, S // I32_BYTES], I32, "v2_scales")
+        rows = kept([P, 2 * S], U8, "rows")
+        planes = [kept([P, S // I32_BYTES], I32, "planes0"), kept([P, 2 * S // I32_BYTES], I32, "planes1")]
 
         raw_w1 = kept([P, PACK, H], F32, "raw_w1")
         raw = {name: kept([P, PACK, KP], F32, "raw_" + name) for name in W2_PIECES}
         raw["w1_0"], raw["w1_1"] = raw_w1[:, :, 0:KP], raw_w1[:, :, KP:H]
-        w_codes = {name: kept([P, KP], U32, "codes_" + name) for name in PIECES if name != "w1_1"}
+        w_codes = {name: kept([P, KP], U32, "codes_" + name) for name in PIECES}
         w_scales = {name: kept([P, KP], U8, "scales_" + name) for name in PIECES}
         disc = {(a, hf): kept([P, PACK, HALF], F32, f"disc{a}{hf}") for a in range(2) for hf in range(2)}
         h_codes = {(a, hf): kept([P, HALF], U32, f"h_codes{a}{hf}") for a, hf in ((0, 0), (1, 0), (1, 1))}
         h_scales = {(a, hf): kept([P, HALF], U8, f"h_scales{a}{hf}") for a in range(2) for hf in range(2)}
-        rounded, values = {}, {}
+        rounded, values, cash_bank = {}, {}, {}
 
         nc.gpsimd.memset(curve_scales[:], 0)
         nc.vector.memset(cash_scales[:], 0)
+        nc.vector.memset(planes[1][:], 0)
+        nc.vector.memset(planes[0][:], 0)
         nc.vector.memset(shift_scales[:], 0)
-        nc.vector.memset(v2_scales[:], 0)
 
         def load_words(tile, words):
             nc.sync.dma_start(out=tile[:], in_=words.rearrange("p t i -> p (t i)").bitcast(I32))
@@ -89,13 +89,13 @@ def tile_list_scenario_cashflow_values_kernel(
             src = w2[g * KP : (g + 1) * KP, a * KP + c0 : a * KP + c1]
             nc.sync.dma_start(out=raw[name][:, :, c0:c1], in_=src.rearrange("(p j) c -> p j c", j=PACK))
 
-        def place_cash_scales(rows):
-            for s in rows:
-                for g in range(2):
-                    nc.sync.dma_start(
-                        out=v2_scales[SCALE_ROWS * (g + 1) + s : P : QUADRANT, :],
-                        in_=v2_rows[:].bitcast(I32)[4 * (BLOCKS * g + s) : 4 * BLOCKS * (g + 1) : 4 * SCALE_ROWS, :],
-                    )
+        def place_scales(g):
+            c0 = 0 if g == 1 else S // I32_BYTES
+            for s in range(SCALE_ROWS):
+                nc.sync.dma_start(
+                    out=planes[g][SCALE_ROWS * (g + 1) + s : P : QUADRANT, :],
+                    in_=rows[:].bitcast(I32)[4 * (BLOCKS * g + s) : 4 * BLOCKS * (g + 1) : 4 * SCALE_ROWS, c0:],
+                )
 
         def gather(dst, window, offsets, j0, j1):
             nc.vector.tensor_copy(dst[:, j0:j1], window.indirect(offsets[:, j0 // LIST_GROUP : j1 // LIST_GROUP]))
@@ -125,33 +125,39 @@ def tile_list_scenario_cashflow_values_kernel(
             name = f"w1_{a}"
             cols = slice(hf * HALF, (hf + 1) * HALF)
             for t in range(PACK):
-                bank = psum.tile([P, HALF], F32, name=f"wide{t % DISCOUNT_BANKS}", bufs=1)
+                bank = psum.tile([P, HALF], F32, name=f"wide{((2 * a + hf) * PACK + t) % DISCOUNT_BANKS}", bufs=1)
                 nc.tensor.matmul_mx(
                     out=bank[:],
                     lhsT=w_codes[name][:, t * P : (t + 1) * P].bitcast(FP8X4),
                     lhsT_scale=w_scales[name][:, t * P : (t + 1) * P],
                     rhs=v_words[:, cols].bitcast(FP8X4),
-                    rhs_scale=v_scales[:, cols],
+                    rhs_scale=planes[1][:].bitcast(U8)[2 * SCALE_ROWS : P, cols],
                     start=True,
                     stop=True,
                 )
                 nc.scalar.activation(out=disc[a, hf][:, t, :], in_=bank[:], func=EXP, bias=bias[:, a, t : t + 1])
 
-        def present_value(a, ch):
+        def cashflow_pass(a, ch, g):
             cols = slice(ch * CH, (ch + 1) * CH)
-            bank = psum.tile([P, PACK, CH], F32, name="narrow")
+            if g == 0:
+                cash_bank[a, ch] = psum.tile([P, PACK, CH], F32, name="narrow")
+            name = f"w2_{a}{g}"
             for t in range(PACK):
-                for g in range(2):
-                    name = f"w2_{a}{g}"
-                    nc.tensor.matmul_mx(
-                        out=bank[:, t, :],
-                        lhsT=w_codes[name][:, t * P : (t + 1) * P].bitcast(FP8X4),
-                        lhsT_scale=w_scales[name][:, t * P : (t + 1) * P],
-                        rhs=v2_words[g][:, cols].bitcast(FP8X4),
-                        rhs_scale=v2_scales[:].bitcast(U8)[SCALE_ROWS * (g + 1) : P, cols],
-                        start=(g == 0),
-                        stop=(g == 1),
-                    )
+                nc.tensor.matmul_mx(
+                    out=cash_bank[a, ch][:, t, :],
+                    lhsT=w_codes[name][:, t * P : (t + 1) * P].bitcast(FP8X4),
+                    lhsT_scale=w_scales[name][:, t * P : (t + 1) * P],
+                    rhs=v2_words[g][:, cols].bitcast(FP8X4),
+                    rhs_scale=planes[g][:].bitcast(U8)[SCALE_ROWS * (g + 1) : P, g * S :][:, cols],
+                    start=(g == 0 and t == 0),
+                    stop=(g == 1 and t == PACK - 1),
+                )
+
+        def present_value(a, ch):
+            for g in range(2):
+                if g == 1 or (a, ch) not in cash_bank:
+                    cashflow_pass(a, ch, g)
+            bank = cash_bank[a, ch]
             hf, j0 = divmod(ch * CH, HALF)
             first, end = [run for run in RUNS[a] if run[0] <= ch < run[1]][0]
             if ch == first:
@@ -203,50 +209,45 @@ def tile_list_scenario_cashflow_values_kernel(
             nc.sync.dma_start(out=out[u0 * P : u1 * P, j0:j1].rearrange("(u p) j -> p u j", p=P), in_=result)
 
         load_words(curve_words, tab_words[0])
-        nc.sync.dma_start(idx[:], offs)
-        for s in range(SCALE_ROWS):
-            nc.sync.dma_start(
-                out=curve_scales[s:P:QUADRANT, :], in_=tab_scales[0].bitcast(I32)[s:BLOCKS:SCALE_ROWS, :]
-            )
-        nc.sync.dma_start(out=raw_w1[:], in_=w1.rearrange("(p j) c -> p j c", j=PACK))
         nc.sync.dma_start(idx2[:], offs2)
         nc.sync.dma_start(out=cash_scales[0:P:4, :], in_=tab2_scales.bitcast(I32).rearrange("g q t -> (g q) t"))
-        nc.sync.dma_start(out=bias[:], in_=b1.rearrange("(a p t) -> p a t", a=2, t=PACK))
+        nc.sync.dma_start(out=curve_scales[4 * BLOCKS : P : 4, :], in_=tab_scales[0].bitcast(I32))
+        nc.sync.dma_start(idx[:], offs)
+        nc.sync.dma_start(out=raw_w1[:], in_=w1.rearrange("(p j) c -> p j c", j=PACK))
+        nc.sync.dma_start(out=bias[:, :, 0:PACK], in_=b1.rearrange("(a p t) -> p a t", a=2, t=PACK))
         load_words(cash_words[0], tab2_words[0])
+
+        gather(rows[:, S:], cash_scales[:].bitcast(U8), idx2, 0, S)
+        gather(rows[:, 0:S], curve_scales[:].bitcast(U8), idx, 0, S)
+        gather(v_words, curve_words[:].bitcast(U32), idx, 0, S)
+
+        place_scales(1)
+        load_w2("w2_00")
+        load_w2("w2_01")
+        load_words(cash_words[1], tab2_words[1])
+        place_scales(0)
+        load_w2("w2_10")
         for s in range(SCALE_ROWS):
             nc.sync.dma_start(
                 out=shift_scales[s:P:QUADRANT, :, :],
                 in_=w4_scales.bitcast(I32)[:, s:BLOCKS:SCALE_ROWS, :].rearrange("a q n -> q a n"),
             )
-        load_w2("w2_00")
-        load_w2("w2_01")
-
-        gather(v_words, curve_words[:].bitcast(U32), idx, 0, S)
-        gather(v_scales, curve_scales[:].bitcast(U8), idx, 0, S)
-        gather(v2_rows, cash_scales[:].bitcast(U8), idx2, 0, S)
-        for a in range(2):
-            round_piece(f"w1_{a}", nc.scalar.copy)
-        quantize_piece("w1_0")
-        for hf in range(2):
-            discount(0, hf)
-
-        place_cash_scales((0, 1))
-        load_words(cash_words[1], tab2_words[1])
-        place_cash_scales((2, 3))
-        load_w2("w2_10")
         load_w2("w2_11", 0, KP // 2)
         load_w2("w2_11", KP // 2, KP)
         nc.sync.dma_start(out=shift_words[:], in_=w4_words.bitcast(I32).rearrange("a p n -> p a n"))
         with nc.allow_non_contiguous_dma(reason="one rate to a partition and output tile"):
             nc.sync.dma_start(out=rate[:], in_=fx.rearrange("(u p) -> p u", p=P))
 
+        for a in range(2):
+            round_piece(f"w1_{a}", nc.scalar.copy)
+            quantize_piece(f"w1_{a}")
+        for a in range(2):
+            for hf in range(2):
+                discount(a, hf)
+
         gather(v2_words[0], cash_words[0][:].bitcast(U32), idx2, 0, S)
         round_piece("w2_00", nc.vector.tensor_copy)
-        w_codes["w1_1"] = kept([P, KP], U32, "raw_w2_00")
-        quantize_piece("w1_1")
         quantize_piece("w2_00")
-        for hf in range(2):
-            discount(1, hf)
         round_piece("w2_01", nc.vector.tensor_copy)
         quantize_piece("w2_01")
         for hf in range(2):
@@ -255,6 +256,8 @@ def tile_list_scenario_cashflow_values_kernel(
         round_piece("w2_11", nc.scalar.copy, (0, KP // 2, KP))
         h_codes[0, 1] = kept([P, HALF], U32, "raw_w2_11")
 
+        for ch in range(4):
+            cashflow_pass(0, ch, 0)
         present_value(0, 0)
         present_value(0, 1)
         quantize_piece("w2_10")

@@ -34,7 +34,7 @@ DISCOUNT_BANKS = 3
 W2_PIECES = {"w2_00": (0, 0), "w2_01": (1, 0), "w2_10": (0, 1), "w2_11": (1, 1)}
 PIECES = ["w1_0", "w1_1", *W2_PIECES]
 
-RUNS = {0: [(0, 4), (4, 6), (6, 7), (7, 8)], 1: [(0, 2), (2, 4), (4, 5), (5, 6), (6, 7), (7, 8)]}
+RUNS = {0: [(0, 4), (4, 6), (6, 7), (7, 8)], 1: [(0, 2), (2, 4), (4, 6), (6, 7), (7, 8)]}
 RUN_TILE = {(0, 6): "last_rounded", (0, 7): "values10"}
 
 
@@ -73,7 +73,8 @@ def tile_list_scenario_cashflow_values_kernel(
         disc = {(a, hf): kept([P, PACK, HALF], F32, f"disc{a}{hf}") for a in range(2) for hf in range(2)}
         h_codes = {(a, hf): kept([P, HALF], U32, f"h_codes{a}{hf}") for a, hf in ((0, 0), (1, 0), (1, 1))}
         h_scales = {(a, hf): kept([P, HALF], U8, f"h_scales{a}{hf}") for a in range(2) for hf in range(2)}
-        rounded, values, cash_bank = {}, {}, {}
+        rounded, values, cash_bank, out_bank = {}, {}, {}, {}
+        passes_done = set()
 
         nc.gpsimd.memset(curve_scales[:], 0)
         nc.vector.memset(cash_scales[:], 0)
@@ -140,7 +141,9 @@ def tile_list_scenario_cashflow_values_kernel(
         def cashflow_pass(a, ch, g):
             cols = slice(ch * CH, (ch + 1) * CH)
             if g == 0:
-                cash_bank[a, ch] = psum.tile([P, PACK, CH], F32, name="narrow")
+                turn = ch % 4 if a == 0 else ch % 3
+                cash_bank[a, ch] = psum.tile([P, PACK, CH], F32, name=f"narrow{turn}", bufs=1)
+            passes_done.add((a, ch, g))
             name = f"w2_{a}{g}"
             for t in range(PACK):
                 nc.tensor.matmul_mx(
@@ -153,10 +156,13 @@ def tile_list_scenario_cashflow_values_kernel(
                     stop=(g == 1 and t == PACK - 1),
                 )
 
-        def present_value(a, ch):
+        def cashflow(a, ch):
             for g in range(2):
-                if g == 1 or (a, ch) not in cash_bank:
+                if (a, ch, g) not in passes_done:
                     cashflow_pass(a, ch, g)
+
+        def present_value(a, ch):
+            cashflow(a, ch)
             bank = cash_bank[a, ch]
             hf, j0 = divmod(ch * CH, HALF)
             first, end = [run for run in RUNS[a] if run[0] <= ch < run[1]][0]
@@ -180,30 +186,47 @@ def tile_list_scenario_cashflow_values_kernel(
                 in_=values[a, first][:].rearrange("p j t -> p (j t)"),
             )
 
-        def scenario_pass(dst, u, a, hf, j0, j1):
-            nc.tensor.matmul_mx(
-                out=dst,
-                lhsT=shift_words[:, a, :].bitcast(U8)[:, 2 * P * u : 2 * P * (u + 1)].bitcast(FP4X4),
-                lhsT_scale=shift_scales[:, a, :].bitcast(U8)[:, P * u : P * (u + 1)],
-                rhs=h_codes[a, hf][:, j0:j1].bitcast(FP8X4),
-                rhs_scale=h_scales[a, hf][:, j0:j1],
-                start=(a == 0),
-                stop=(a == 1),
-            )
+        def scenario_pass(a, name, u0, u1, ch0, ch1):
+            if a == 0:
+                out_bank[u0, ch0] = psum.tile([P, u1 - u0, (ch1 - ch0) * CH], F32, name=name, bufs=1)
+            for ch in range(ch0, ch1):
+                hf, j0 = divmod(ch * CH, HALF)
+                for u in range(u0, u1):
+                    nc.tensor.matmul_mx(
+                        out=out_bank[u0, ch0][:, u - u0, (ch - ch0) * CH : (ch - ch0 + 1) * CH],
+                        lhsT=shift_words[:, a, :].bitcast(U8)[:, 2 * P * u : 2 * P * (u + 1)].bitcast(FP4X4),
+                        lhsT_scale=shift_scales[:, a, :].bitcast(U8)[:, P * u : P * (u + 1)],
+                        rhs=h_codes[a, hf][:, j0 : j0 + CH].bitcast(FP8X4),
+                        rhs_scale=h_scales[a, hf][:, j0 : j0 + CH],
+                        start=(a == 0 and ch == ch0 and u == u0),
+                        stop=(a == 1 and ch == ch1 - 1 and u == u1 - 1),
+                    )
 
-        def scenario_bank(ch, u0, u1):
-            hf, j0 = divmod(ch * CH, HALF)
-            bank = psum.tile([P, u1 - u0, CH], F32, name="narrow")
-            for u in range(u0, u1):
-                for a in range(2):
-                    scenario_pass(bank[:, u - u0, :], u, a, hf, j0, j0 + CH)
-            return bank
-
-        def apply_rate_on_scalar(result, bank, u0, u1):
-            for u in range(u0, u1):
-                nc.scalar.activation(
-                    out=result[:, u - u0, :], in_=bank[:, u - u0, :], func=COPY, scale=rate[:, u : u + 1]
+        def leave(bank, b0, u0, u1, ch0, ch1, on_vector=False):
+            width = (ch1 - ch0) * CH
+            result = kept([P, u1 - u0, width], F32, f"result{u0}{ch0}")
+            if on_vector:
+                nc.vector.tensor_tensor(
+                    out=result[:],
+                    in0=bank[:, b0 : b0 + u1 - u0, :],
+                    in1=rate[:, u0:u1].unsqueeze(2).to_broadcast([P, u1 - u0, width]),
+                    op=MULT,
                 )
+            else:
+                for u in range(u0, u1):
+                    nc.scalar.activation(
+                        out=result[:, u - u0, :], in_=bank[:, b0 + u - u0, :], func=COPY, scale=rate[:, u : u + 1]
+                    )
+            store(result[:], u0, u1, ch0 * CH, ch1 * CH)
+
+        def open_pair(ch, first_bank):
+            for i in range(2):
+                scenario_pass(0, f"wide{first_bank + i}", 2 * i, 2 * i + 2, ch, ch + 2)
+
+        def close_pair(ch):
+            for i in range(2):
+                scenario_pass(1, None, 2 * i, 2 * i + 2, ch, ch + 2)
+                leave(out_bank[2 * i, ch], 0, 2 * i, 2 * i + 2, ch, ch + 2)
 
         def store(result, u0, u1, j0, j1):
             nc.sync.dma_start(out=out[u0 * P : u1 * P, j0:j1].rearrange("(u p) j -> p u j", p=P), in_=result)
@@ -223,18 +246,18 @@ def tile_list_scenario_cashflow_values_kernel(
 
         place_scales(1)
         load_w2("w2_00")
-        load_w2("w2_01")
-        load_words(cash_words[1], tab2_words[1])
-        place_scales(0)
-        load_w2("w2_10")
         for s in range(SCALE_ROWS):
             nc.sync.dma_start(
                 out=shift_scales[s:P:QUADRANT, :, :],
                 in_=w4_scales.bitcast(I32)[:, s:BLOCKS:SCALE_ROWS, :].rearrange("a q n -> q a n"),
             )
+        load_w2("w2_01")
+        load_words(cash_words[1], tab2_words[1])
+        place_scales(0)
+        load_w2("w2_10")
+        nc.sync.dma_start(out=shift_words[:], in_=w4_words.bitcast(I32).rearrange("a p n -> p a n"))
         load_w2("w2_11", 0, KP // 2)
         load_w2("w2_11", KP // 2, KP)
-        nc.sync.dma_start(out=shift_words[:], in_=w4_words.bitcast(I32).rearrange("a p n -> p a n"))
         with nc.allow_non_contiguous_dma(reason="one rate to a partition and output tile"):
             nc.sync.dma_start(out=rate[:], in_=fx.rearrange("(u p) -> p u", p=P))
 
@@ -256,7 +279,7 @@ def tile_list_scenario_cashflow_values_kernel(
         round_piece("w2_11", nc.scalar.copy, (0, KP // 2, KP))
         h_codes[0, 1] = kept([P, HALF], U32, "raw_w2_11")
 
-        for ch in range(4):
+        for ch in range(2):
             cashflow_pass(0, ch, 0)
         present_value(0, 0)
         present_value(0, 1)
@@ -267,51 +290,45 @@ def tile_list_scenario_cashflow_values_kernel(
         present_value(0, 4)
         quantize_run(0, 0)
         present_value(0, 5)
+        cashflow(0, 6)
+        cashflow(0, 7)
+        open_pair(0, 0)
+        open_pair(2, 2)
+        cashflow_pass(1, 0, 0)
+        cashflow_pass(1, 1, 0)
+        cashflow(1, 0)
+        cashflow(1, 1)
         present_value(0, 6)
-        quantize_run(0, 4)
-        wide = [psum.tile([P, HALF], F32, name=f"wide{u}", bufs=1) for u in range(OUT_TILES)]
-        for u in range(OUT_TILES):
-            scenario_pass(wide[u][:], u, 0, 0, 0, HALF)
-
-        present_value(1, 0)
-        present_value(1, 1)
-        present_value(1, 2)
+        cashflow(1, 2)
+        for ch in range(3):
+            present_value(1, ch)
+            cashflow(1, ch + 3)
         quantize_run(1, 0)
+        close_pair(0)
         present_value(1, 3)
-        quantize_run(0, 6)
+        cashflow(1, 6)
+        quantize_run(0, 4)
         quantize_run(1, 2)
-        present_value(0, 7)
+        close_pair(2)
         present_value(1, 4)
-        quantize_run(0, 7)
-        for u in range(OUT_TILES):
-            scenario_pass(wide[u][:], u, 1, 0, 0, HALF)
-            result = kept([P, 1, HALF], F32, f"result_wide{u}")
-            nc.scalar.activation(out=result[:, 0, :], in_=wide[u][:], func=COPY, scale=rate[:, u : u + 1])
-            store(result[:], u, u + 1, 0, HALF)
-
+        cashflow(1, 7)
+        open_pair(4, 0)
+        quantize_run(0, 6)
         present_value(1, 5)
+        present_value(0, 7)
         quantize_run(1, 4)
+        close_pair(4)
+        scenario_pass(0, "wide2", 0, OUT_TILES, 6, 7)
         present_value(1, 6)
-        quantize_run(1, 5)
-        pair = kept([P, OUT_TILES, 2 * CH], F32, "result_pair")
-        apply_rate_on_scalar(pair[:, :, 0:CH], scenario_bank(4, 0, OUT_TILES), 0, OUT_TILES)
-        present_value(1, 7)
+        quantize_run(0, 7)
         quantize_run(1, 6)
-        apply_rate_on_scalar(pair[:, :, CH : 2 * CH], scenario_bank(5, 0, OUT_TILES), 0, OUT_TILES)
-        store(pair[:], 0, OUT_TILES, 4 * CH, 6 * CH)
+        scenario_pass(1, None, 0, OUT_TILES, 6, 7)
+        scenario_pass(0, "wide3", 0, 2, 7, 8)
+        scenario_pass(0, "narrow3", 2, 4, 7, 8)
+        for u0 in (0, 2):
+            leave(out_bank[0, 6], u0, u0, u0 + 2, 6, 7)
+        present_value(1, 7)
         quantize_run(1, 7)
-        single = kept([P, OUT_TILES, CH], F32, "result_single")
-        apply_rate_on_scalar(single[:], scenario_bank(6, 0, OUT_TILES), 0, OUT_TILES)
-        store(single[:], 0, OUT_TILES, 6 * CH, 7 * CH)
-        mid = OUT_TILES // 2
-        upper = kept([P, mid, CH], F32, "result_upper")
-        nc.vector.tensor_tensor(
-            out=upper[:],
-            in0=scenario_bank(7, 0, mid)[:],
-            in1=rate[:, 0:mid].unsqueeze(2).to_broadcast([P, mid, CH]),
-            op=MULT,
-        )
-        store(upper[:], 0, mid, 7 * CH, S)
-        lower = kept([P, mid, CH], F32, "result_lower")
-        apply_rate_on_scalar(lower[:], scenario_bank(7, mid, OUT_TILES), mid, OUT_TILES)
-        store(lower[:], mid, OUT_TILES, 7 * CH, S)
+        for u0 in (0, 2):
+            scenario_pass(1, None, u0, u0 + 2, 7, 8)
+            leave(out_bank[u0, 7], 0, u0, u0 + 2, 7, 8, on_vector=(u0 == 2))

@@ -29,13 +29,13 @@ HALF = 512
 CH = 128
 LINE = 4
 OUT_TILES = N // P
+BANKS = 8
 DISCOUNT_BANKS = 3
 
 W2_PIECES = {"w2_00": (0, 0), "w2_01": (1, 0), "w2_10": (0, 1), "w2_11": (1, 1)}
 PIECES = ["w1_0", "w1_1", *W2_PIECES]
 
-RUNS = {0: [(0, 4), (4, 6), (6, 7), (7, 8)], 1: [(0, 2), (2, 4), (4, 6), (6, 7), (7, 8)]}
-RUN_TILE = {(0, 6): "last_rounded", (0, 7): "values10"}
+RUNS = {0: [(0, 4), (4, 7), (7, 8)], 1: [(0, 2), (2, 4), (4, 6), (6, 7), (7, 8)]}
 
 
 def tile_list_scenario_cashflow_values_kernel(
@@ -45,7 +45,7 @@ def tile_list_scenario_cashflow_values_kernel(
     with ExitStack() as ctx:
         keep = ctx.enter_context(tc.tile_pool(name="keep", bufs=1))
         ring = ctx.enter_context(tc.tile_pool(name="ring", bufs=3))
-        psum = ctx.enter_context(tc.psum_pool(name="psum", bufs=4))
+        psum = ctx.enter_context(tc.psum_pool(name="psum", bufs=1))
 
         def kept(shape, dtype, name):
             return keep.tile(shape, dtype, name=name, align_bytes=64)
@@ -74,7 +74,6 @@ def tile_list_scenario_cashflow_values_kernel(
         h_codes = {(a, hf): kept([P, HALF], U32, f"h_codes{a}{hf}") for a, hf in ((0, 0), (1, 0), (1, 1))}
         h_scales = {(a, hf): kept([P, HALF], U8, f"h_scales{a}{hf}") for a in range(2) for hf in range(2)}
         rounded, values, cash_bank, out_bank = {}, {}, {}, {}
-        passes_done = set()
 
         nc.gpsimd.memset(curve_scales[:], 0)
         nc.vector.memset(cash_scales[:], 0)
@@ -126,7 +125,7 @@ def tile_list_scenario_cashflow_values_kernel(
             name = f"w1_{a}"
             cols = slice(hf * HALF, (hf + 1) * HALF)
             for t in range(PACK):
-                bank = psum.tile([P, HALF], F32, name=f"wide{((2 * a + hf) * PACK + t) % DISCOUNT_BANKS}", bufs=1)
+                bank = psum.tile([P, HALF], F32, name=f"bank{BANKS - 1 - ((2 * a + hf) * PACK + t) % DISCOUNT_BANKS}")
                 nc.tensor.matmul_mx(
                     out=bank[:],
                     lhsT=w_codes[name][:, t * P : (t + 1) * P].bitcast(FP8X4),
@@ -138,14 +137,12 @@ def tile_list_scenario_cashflow_values_kernel(
                 )
                 nc.scalar.activation(out=disc[a, hf][:, t, :], in_=bank[:], func=EXP, bias=bias[:, a, t : t + 1])
 
-        def cashflow_pass(a, ch, g):
+        def cashflow_pass(a, ch, g, t0=0, t1=PACK):
             cols = slice(ch * CH, (ch + 1) * CH)
-            if g == 0:
-                turn = ch % 4 if a == 0 else ch % 3
-                cash_bank[a, ch] = psum.tile([P, PACK, CH], F32, name=f"narrow{turn}", bufs=1)
-            passes_done.add((a, ch, g))
+            if (g, t0) == (0, 0):
+                cash_bank[a, ch] = psum.tile([P, PACK, CH], F32, name=f"bank{ch if a == 0 else 4 + ch % 4}")
             name = f"w2_{a}{g}"
-            for t in range(PACK):
+            for t in range(t0, t1):
                 nc.tensor.matmul_mx(
                     out=cash_bank[a, ch][:, t, :],
                     lhsT=w_codes[name][:, t * P : (t + 1) * P].bitcast(FP8X4),
@@ -158,16 +155,14 @@ def tile_list_scenario_cashflow_values_kernel(
 
         def cashflow(a, ch):
             for g in range(2):
-                if (a, ch, g) not in passes_done:
-                    cashflow_pass(a, ch, g)
+                cashflow_pass(a, ch, g)
 
         def present_value(a, ch):
-            cashflow(a, ch)
             bank = cash_bank[a, ch]
             hf, j0 = divmod(ch * CH, HALF)
             first, end = [run for run in RUNS[a] if run[0] <= ch < run[1]][0]
             if ch == first:
-                name = RUN_TILE.get((a, first), f"values{a}{first}")
+                name = "last_rounded" if (a, first) == (0, 7) else f"values{a}{first}"
                 values[a, first] = kept([P, (end - first) * CH, PACK], BF16, name)
             i0 = (ch - first) * CH
             nc.vector.tensor_tensor(
@@ -186,21 +181,21 @@ def tile_list_scenario_cashflow_values_kernel(
                 in_=values[a, first][:].rearrange("p j t -> p (j t)"),
             )
 
-        def scenario_pass(a, name, u0, u1, ch0, ch1):
+        def scenario_pass(a, bank, u0, u1, ch0, ch1):
+            width = (ch1 - ch0) * CH
             if a == 0:
-                out_bank[u0, ch0] = psum.tile([P, u1 - u0, (ch1 - ch0) * CH], F32, name=name, bufs=1)
-            for ch in range(ch0, ch1):
-                hf, j0 = divmod(ch * CH, HALF)
-                for u in range(u0, u1):
-                    nc.tensor.matmul_mx(
-                        out=out_bank[u0, ch0][:, u - u0, (ch - ch0) * CH : (ch - ch0 + 1) * CH],
-                        lhsT=shift_words[:, a, :].bitcast(U8)[:, 2 * P * u : 2 * P * (u + 1)].bitcast(FP4X4),
-                        lhsT_scale=shift_scales[:, a, :].bitcast(U8)[:, P * u : P * (u + 1)],
-                        rhs=h_codes[a, hf][:, j0 : j0 + CH].bitcast(FP8X4),
-                        rhs_scale=h_scales[a, hf][:, j0 : j0 + CH],
-                        start=(a == 0 and ch == ch0 and u == u0),
-                        stop=(a == 1 and ch == ch1 - 1 and u == u1 - 1),
-                    )
+                out_bank[u0, ch0] = psum.tile([P, u1 - u0, width], F32, name=f"bank{bank}")
+            hf, j0 = divmod(ch0 * CH, HALF)
+            for u in range(u0, u1):
+                nc.tensor.matmul_mx(
+                    out=out_bank[u0, ch0][:, u - u0, :],
+                    lhsT=shift_words[:, a, :].bitcast(U8)[:, 2 * P * u : 2 * P * (u + 1)].bitcast(FP4X4),
+                    lhsT_scale=shift_scales[:, a, :].bitcast(U8)[:, P * u : P * (u + 1)],
+                    rhs=h_codes[a, hf][:, j0 : j0 + width].bitcast(FP8X4),
+                    rhs_scale=h_scales[a, hf][:, j0 : j0 + width],
+                    start=(a == 0 and u == u0),
+                    stop=(a == 1 and u == u1 - 1),
+                )
 
         def leave(bank, b0, u0, u1, ch0, ch1, on_vector=False):
             width = (ch1 - ch0) * CH
@@ -221,7 +216,7 @@ def tile_list_scenario_cashflow_values_kernel(
 
         def open_pair(ch, first_bank):
             for i in range(2):
-                scenario_pass(0, f"wide{first_bank + i}", 2 * i, 2 * i + 2, ch, ch + 2)
+                scenario_pass(0, first_bank + i, 2 * i, 2 * i + 2, ch, ch + 2)
 
         def close_pair(ch):
             for i in range(2):
@@ -277,58 +272,64 @@ def tile_list_scenario_cashflow_values_kernel(
             gather(v2_words[1], cash_words[1][:].bitcast(U32), idx2, hf * HALF, (hf + 1) * HALF)
         round_piece("w2_10", nc.scalar.copy)
         round_piece("w2_11", nc.scalar.copy, (0, KP // 2, KP))
-        h_codes[0, 1] = kept([P, HALF], U32, "raw_w2_11")
 
         for ch in range(2):
             cashflow_pass(0, ch, 0)
-        present_value(0, 0)
-        present_value(0, 1)
-        quantize_piece("w2_10")
-        present_value(0, 2)
-        present_value(0, 3)
-        quantize_piece("w2_11", calls=2)
-        present_value(0, 4)
+        for ch in range(2):
+            cashflow_pass(0, ch, 1)
+        for ch in range(2, 8):
+            cashflow(0, ch)
+        for ch in range(5):
+            present_value(0, ch)
         quantize_run(0, 0)
-        present_value(0, 5)
-        cashflow(0, 6)
-        cashflow(0, 7)
         open_pair(0, 0)
         open_pair(2, 2)
+        quantize_piece("w2_10")
         cashflow_pass(1, 0, 0)
-        cashflow_pass(1, 1, 0)
-        cashflow(1, 0)
-        cashflow(1, 1)
-        present_value(0, 6)
-        cashflow(1, 2)
-        for ch in range(3):
-            present_value(1, ch)
-            cashflow(1, ch + 3)
+        for ch in range(5, 7):
+            present_value(0, ch)
+            cashflow_pass(1, ch - 4, 0)
+
+        quantize_piece("w2_11", calls=2)
+        for t0 in (0, 2):
+            for ch in range(2):
+                cashflow_pass(1, ch, 1, t0, t0 + 2)
+        cashflow_pass(1, 2, 1)
+        present_value(0, 7)
+        cashflow(1, 3)
+
+        present_value(1, 0)
+        cashflow(1, 4)
+        present_value(1, 1)
+        h_codes[0, 1] = kept([P, HALF], U32, "raw_w2_11")
+        quantize_run(0, 4)
         quantize_run(1, 0)
         close_pair(0)
-        present_value(1, 3)
+        cashflow(1, 5)
+        present_value(1, 2)
         cashflow(1, 6)
-        quantize_run(0, 4)
+        present_value(1, 3)
+        quantize_run(0, 7)
         quantize_run(1, 2)
         close_pair(2)
-        present_value(1, 4)
         cashflow(1, 7)
-        open_pair(4, 0)
-        quantize_run(0, 6)
+        present_value(1, 4)
         present_value(1, 5)
-        present_value(0, 7)
+        open_pair(4, 0)
+        present_value(1, 6)
         quantize_run(1, 4)
         close_pair(4)
-        scenario_pass(0, "wide2", 0, OUT_TILES, 6, 7)
-        present_value(1, 6)
-        quantize_run(0, 7)
         quantize_run(1, 6)
-        scenario_pass(1, None, 0, OUT_TILES, 6, 7)
-        scenario_pass(0, "wide3", 0, 2, 7, 8)
-        scenario_pass(0, "narrow3", 2, 4, 7, 8)
-        for u0 in (0, 2):
-            leave(out_bank[0, 6], u0, u0, u0 + 2, 6, 7)
+        for i in range(2):
+            scenario_pass(0, 4 + i, 2 * i, 2 * i + 2, 6, 7)
+        for i in range(2):
+            scenario_pass(1, None, 2 * i, 2 * i + 2, 6, 7)
+        for i in range(2):
+            scenario_pass(0, 2 + i, 2 * i, 2 * i + 2, 7, 8)
         present_value(1, 7)
+        leave(out_bank[0, 6], 0, 0, 2, 6, 7)
         quantize_run(1, 7)
+        leave(out_bank[2, 6], 0, 2, 4, 6, 7, on_vector=True)
         for u0 in (0, 2):
             scenario_pass(1, None, u0, u0 + 2, 7, 8)
             leave(out_bank[u0, 7], 0, u0, u0 + 2, 7, 8, on_vector=(u0 == 2))

@@ -35,7 +35,7 @@ DISCOUNT_BANKS = 3
 W2_PIECES = {"w2_00": (0, 0), "w2_01": (1, 0), "w2_10": (0, 1), "w2_11": (1, 1)}
 PIECES = ["w1_0", "w1_1", *W2_PIECES]
 
-RUNS = {0: [(0, 4), (4, 7), (7, 8)], 1: [(0, 2), (2, 4), (4, 6), (6, 7), (7, 8)]}
+RUNS = {0: [(0, 4), (4, 6), (6, 7), (7, 8)], 1: [(0, 2), (2, 4), (4, 6), (6, 7), (7, 8)]}
 
 
 def tile_list_scenario_cashflow_values_kernel(
@@ -298,38 +298,31 @@ def tile_list_scenario_cashflow_values_kernel(
         present_value(0, 7)
         cashflow(1, 3)
 
-        present_value(1, 0)
-        cashflow(1, 4)
-        present_value(1, 1)
+        for ch in range(2):
+            present_value(1, ch)
+            cashflow(1, ch + 4)
         h_codes[0, 1] = kept([P, HALF], U32, "raw_w2_11")
         quantize_run(0, 4)
         quantize_run(1, 0)
         close_pair(0)
-        cashflow(1, 5)
-        present_value(1, 2)
-        cashflow(1, 6)
-        present_value(1, 3)
-        quantize_run(0, 7)
+        for ch in range(2, 4):
+            present_value(1, ch)
+            cashflow(1, ch + 4)
+        quantize_run(0, 6)
         quantize_run(1, 2)
         close_pair(2)
-        cashflow(1, 7)
         present_value(1, 4)
-        present_value(1, 5)
         open_pair(4, 0)
-        present_value(1, 6)
+        present_value(1, 5)
+        quantize_run(0, 7)
         quantize_run(1, 4)
         close_pair(4)
-        quantize_run(1, 6)
-        for i in range(2):
-            scenario_pass(0, 4 + i, 2 * i, 2 * i + 2, 6, 7)
-        for i in range(2):
-            scenario_pass(1, None, 2 * i, 2 * i + 2, 6, 7)
-        for i in range(2):
-            scenario_pass(0, 2 + i, 2 * i, 2 * i + 2, 7, 8)
+        present_value(1, 6)
+        for u, bank in enumerate((4, 5, 2, 6)):
+            scenario_pass(0, bank, u, u + 1, 6, 8)
         present_value(1, 7)
-        leave(out_bank[0, 6], 0, 0, 2, 6, 7)
+        quantize_run(1, 6)
         quantize_run(1, 7)
-        leave(out_bank[2, 6], 0, 2, 4, 6, 7, on_vector=True)
-        for u0 in (0, 2):
-            scenario_pass(1, None, u0, u0 + 2, 7, 8)
-            leave(out_bank[u0, 7], 0, u0, u0 + 2, 7, 8, on_vector=(u0 == 2))
+        for u in range(OUT_TILES):
+            scenario_pass(1, None, u, u + 1, 6, 8)
+            leave(out_bank[u, 6], 0, u, u + 1, 6, 8, on_vector=(u % 2 == 1))

@@ -56,7 +56,7 @@ def tile_list_scenario_cashflow_values_kernel(
         curve_scales = kept([P, T // I32_BYTES], I32, "curve_scales")
         cash_words = [kept([P, T2], I32, f"cash_words{g}") for g in range(2)]
         cash_scales = kept([P, T2 // I32_BYTES], I32, "cash_scales")
-        shift_words = kept([P, 2, 2 * N // I32_BYTES], I32, "shift_words")
+        shift_words = [kept([P, 2 * N // I32_BYTES], I32, f"shift_words{a}") for a in range(2)]
         shift_scales = kept([P, 2, N // I32_BYTES], I32, "shift_scales")
         bias = kept([P, 2, 2 * PACK], F32, "bias")
         rate = kept([P, OUT_TILES], F32, "rate")
@@ -100,10 +100,8 @@ def tile_list_scenario_cashflow_values_kernel(
         def gather(dst, window, offsets, j0, j1):
             nc.vector.tensor_copy(dst[:, j0:j1], window.indirect(offsets[:, j0 // LIST_GROUP : j1 // LIST_GROUP]))
 
-        def round_piece(name, copy, cuts=(0, KP)):
-            if name == "w2_11":
-                grouped = kept([P, PACK, P, PACK], BF16, "last_rounded")
-            else:
+        def round_piece(name, copy, cuts=(0, KP), grouped=None):
+            if grouped is None:
                 grouped = ring.tile([P, PACK, P, PACK], BF16, name="grouped", align_bytes=64)
             for c0, c1 in zip(cuts[:-1], cuts[1:]):
                 copy(
@@ -162,9 +160,14 @@ def tile_list_scenario_cashflow_values_kernel(
             hf, j0 = divmod(ch * CH, HALF)
             first, end = [run for run in RUNS[a] if run[0] <= ch < run[1]][0]
             if ch == first:
-                name = "last_rounded" if (a, first) == (0, 7) else f"values{a}{first}"
+                name = {(0, 7): "last_rounded", (1, 6): "values14"}.get((a, first), f"values{a}{first}")
                 values[a, first] = kept([P, (end - first) * CH, PACK], BF16, name)
             i0 = (ch - first) * CH
+            if (a, ch) == (0, 0):
+                parked = kept([P, CH, PACK], F32, "parked")
+                nc.scalar.copy(out=parked[:], in_=bank[:].rearrange("p t j -> p j t"))
+                nc.gpsimd.tensor_tensor(out=values[a, first][:, 0:CH, :], in0=parked[:], in1=woven[:], op=MULT)
+                return
             nc.vector.tensor_tensor(
                 out=values[a, first][:, i0 : i0 + CH, :].rearrange("p (c i) t -> p c t i", i=LINE),
                 in0=bank[:].rearrange("p t (c i) -> p c t i", i=LINE),
@@ -189,7 +192,7 @@ def tile_list_scenario_cashflow_values_kernel(
             for u in range(u0, u1):
                 nc.tensor.matmul_mx(
                     out=out_bank[u0, ch0][:, u - u0, :],
-                    lhsT=shift_words[:, a, :].bitcast(U8)[:, 2 * P * u : 2 * P * (u + 1)].bitcast(FP4X4),
+                    lhsT=shift_words[a][:].bitcast(U8)[:, 2 * P * u : 2 * P * (u + 1)].bitcast(FP4X4),
                     lhsT_scale=shift_scales[:, a, :].bitcast(U8)[:, P * u : P * (u + 1)],
                     rhs=h_codes[a, hf][:, j0 : j0 + width].bitcast(FP8X4),
                     rhs_scale=h_scales[a, hf][:, j0 : j0 + width],
@@ -221,7 +224,8 @@ def tile_list_scenario_cashflow_values_kernel(
         def close_pair(ch):
             for i in range(2):
                 scenario_pass(1, None, 2 * i, 2 * i + 2, ch, ch + 2)
-                leave(out_bank[2 * i, ch], 0, 2 * i, 2 * i + 2, ch, ch + 2)
+                for u in range(2 * i, 2 * i + 2):
+                    leave(out_bank[2 * i, ch], u - 2 * i, u, u + 1, ch, ch + 2)
 
         def store(result, u0, u1, j0, j1):
             nc.sync.dma_start(out=out[u0 * P : u1 * P, j0:j1].rearrange("(u p) j -> p u j", p=P), in_=result)
@@ -250,9 +254,10 @@ def tile_list_scenario_cashflow_values_kernel(
         load_words(cash_words[1], tab2_words[1])
         place_scales(0)
         load_w2("w2_10")
-        nc.sync.dma_start(out=shift_words[:], in_=w4_words.bitcast(I32).rearrange("a p n -> p a n"))
+        nc.sync.dma_start(out=shift_words[0][:], in_=w4_words[0].bitcast(I32))
         load_w2("w2_11", 0, KP // 2)
         load_w2("w2_11", KP // 2, KP)
+        nc.sync.dma_start(out=shift_words[1][:], in_=w4_words[1].bitcast(I32))
         with nc.allow_non_contiguous_dma(reason="one rate to a partition and output tile"):
             nc.sync.dma_start(out=rate[:], in_=fx.rearrange("(u p) -> p u", p=P))
 
@@ -268,10 +273,13 @@ def tile_list_scenario_cashflow_values_kernel(
         quantize_piece("w2_00")
         round_piece("w2_01", nc.vector.tensor_copy)
         quantize_piece("w2_01")
+        woven = kept([P, CH, PACK], F32, "woven")
+        nc.vector.tensor_copy(
+            out=woven[:].rearrange("p (c i) t -> p c t i", i=LINE),
+            in_=disc[0, 0][:, :, 0:CH].rearrange("p t (c i) -> p c t i", i=LINE),
+        )
         for hf in range(2):
             gather(v2_words[1], cash_words[1][:].bitcast(U32), idx2, hf * HALF, (hf + 1) * HALF)
-        round_piece("w2_10", nc.scalar.copy)
-        round_piece("w2_11", nc.scalar.copy, (0, KP // 2, KP))
 
         for ch in range(2):
             cashflow_pass(0, ch, 0)
@@ -279,13 +287,18 @@ def tile_list_scenario_cashflow_values_kernel(
             cashflow_pass(0, ch, 1)
         for ch in range(2, 8):
             cashflow(0, ch)
-        for ch in range(5):
+        present_value(0, 0)
+        round_piece("w2_10", nc.scalar.copy)
+        last_rounded = kept([P, PACK, P, PACK], BF16, "last_rounded")
+        round_piece("w2_11", nc.scalar.copy, (KP // 4, KP // 2, KP), last_rounded)
+        for ch in range(1, 5):
             present_value(0, ch)
         quantize_run(0, 0)
         open_pair(0, 0)
         open_pair(2, 2)
         quantize_piece("w2_10")
         cashflow_pass(1, 0, 0)
+        round_piece("w2_11", nc.vector.tensor_copy, (0, KP // 4), last_rounded)
         for ch in range(5, 7):
             present_value(0, ch)
             cashflow_pass(1, ch - 4, 0)
@@ -298,21 +311,25 @@ def tile_list_scenario_cashflow_values_kernel(
         present_value(0, 7)
         cashflow(1, 3)
 
-        for ch in range(2):
-            present_value(1, ch)
-            cashflow(1, ch + 4)
+        present_value(1, 0)
+        cashflow(1, 4)
+        present_value(1, 1)
+        cashflow_pass(1, 5, 0)
         h_codes[0, 1] = kept([P, HALF], U32, "raw_w2_11")
         quantize_run(0, 4)
         quantize_run(1, 0)
         close_pair(0)
-        for ch in range(2, 4):
-            present_value(1, ch)
-            cashflow(1, ch + 4)
+        cashflow_pass(1, 5, 1)
+        present_value(1, 2)
+        cashflow(1, 6)
+        present_value(1, 3)
+        cashflow_pass(1, 7, 0)
         quantize_run(0, 6)
         quantize_run(1, 2)
         close_pair(2)
-        present_value(1, 4)
         open_pair(4, 0)
+        cashflow_pass(1, 7, 1)
+        present_value(1, 4)
         present_value(1, 5)
         quantize_run(0, 7)
         quantize_run(1, 4)

@@ -29,6 +29,7 @@ HALF = 512
 CH = 128
 LINE = 4
 OUT_TILES = N // P
+AHEAD = (0, 1, 2, 5, 6)
 BANKS = 8
 DISCOUNT_BANKS = 3
 
@@ -123,7 +124,7 @@ def tile_list_scenario_cashflow_values_kernel(
             name = f"w1_{a}"
             cols = slice(hf * HALF, (hf + 1) * HALF)
             for t in range(PACK):
-                bank = psum.tile([P, HALF], F32, name=f"bank{BANKS - 1 - ((2 * a + hf) * PACK + t) % DISCOUNT_BANKS}")
+                bank = psum.tile([P, HALF], F32, name=f"bank{BANKS - 1 - (15 - (2 * a + hf) * PACK - t) % DISCOUNT_BANKS}")
                 nc.tensor.matmul_mx(
                     out=bank[:],
                     lhsT=w_codes[name][:, t * P : (t + 1) * P].bitcast(FP8X4),
@@ -135,9 +136,9 @@ def tile_list_scenario_cashflow_values_kernel(
                 )
                 nc.scalar.activation(out=disc[a, hf][:, t, :], in_=bank[:], func=EXP, bias=bias[:, a, t : t + 1])
 
-        def cashflow_pass(a, ch, g, t0=0, t1=PACK):
+        def cashflow_pass(a, ch, g, t0=0, t1=PACK, first=0):
             cols = slice(ch * CH, (ch + 1) * CH)
-            if (g, t0) == (0, 0):
+            if (g, t0) == (first, 0):
                 cash_bank[a, ch] = psum.tile([P, PACK, CH], F32, name=f"bank{ch if a == 0 else 4 + ch % 4}")
             name = f"w2_{a}{g}"
             for t in range(t0, t1):
@@ -147,8 +148,8 @@ def tile_list_scenario_cashflow_values_kernel(
                     lhsT_scale=w_scales[name][:, t * P : (t + 1) * P],
                     rhs=v2_words[g][:, cols].bitcast(FP8X4),
                     rhs_scale=planes[g][:].bitcast(U8)[SCALE_ROWS * (g + 1) : P, g * S :][:, cols],
-                    start=(g == 0 and t == 0),
-                    stop=(g == 1 and t == PACK - 1),
+                    start=(g == first and t == 0),
+                    stop=(g != first and t == PACK - 1),
                 )
 
         def cashflow(a, ch):
@@ -237,21 +238,21 @@ def tile_list_scenario_cashflow_values_kernel(
         nc.sync.dma_start(idx[:], offs)
         nc.sync.dma_start(out=raw_w1[:], in_=w1.rearrange("(p j) c -> p j c", j=PACK))
         nc.sync.dma_start(out=bias[:, :, 0:PACK], in_=b1.rearrange("(a p t) -> p a t", a=2, t=PACK))
-        load_words(cash_words[0], tab2_words[0])
+        load_words(cash_words[1], tab2_words[1])
 
         gather(rows[:, S:], cash_scales[:].bitcast(U8), idx2, 0, S)
         gather(rows[:, 0:S], curve_scales[:].bitcast(U8), idx, 0, S)
         gather(v_words, curve_words[:].bitcast(U32), idx, 0, S)
 
         place_scales(1)
-        load_w2("w2_00")
+        load_w2("w2_01")
         for s in range(SCALE_ROWS):
             nc.sync.dma_start(
                 out=shift_scales[s:P:QUADRANT, :, :],
                 in_=w4_scales.bitcast(I32)[:, s:BLOCKS:SCALE_ROWS, :].rearrange("a q n -> q a n"),
             )
-        load_w2("w2_01")
-        load_words(cash_words[1], tab2_words[1])
+        load_w2("w2_00")
+        load_words(cash_words[0], tab2_words[0])
         place_scales(0)
         load_w2("w2_10")
         nc.sync.dma_start(out=shift_words[0][:], in_=w4_words[0].bitcast(I32))
@@ -268,25 +269,26 @@ def tile_list_scenario_cashflow_values_kernel(
             for hf in range(2):
                 discount(a, hf)
 
-        gather(v2_words[0], cash_words[0][:].bitcast(U32), idx2, 0, S)
-        round_piece("w2_00", nc.vector.tensor_copy)
-        quantize_piece("w2_00")
+        gather(v2_words[1], cash_words[1][:].bitcast(U32), idx2, 0, S)
         round_piece("w2_01", nc.vector.tensor_copy)
         quantize_piece("w2_01")
+        round_piece("w2_00", nc.vector.tensor_copy)
+        quantize_piece("w2_00")
         woven = kept([P, CH, PACK], F32, "woven")
         nc.vector.tensor_copy(
             out=woven[:].rearrange("p (c i) t -> p c t i", i=LINE),
             in_=disc[0, 0][:, :, 0:CH].rearrange("p t (c i) -> p c t i", i=LINE),
         )
         for hf in range(2):
-            gather(v2_words[1], cash_words[1][:].bitcast(U32), idx2, hf * HALF, (hf + 1) * HALF)
+            gather(v2_words[0], cash_words[0][:].bitcast(U32), idx2, hf * HALF, (hf + 1) * HALF)
 
-        for ch in range(2):
-            cashflow_pass(0, ch, 0)
-        for ch in range(2):
-            cashflow_pass(0, ch, 1)
-        for ch in range(2, 8):
-            cashflow(0, ch)
+        for ch in AHEAD:
+            cashflow_pass(0, ch, 1, first=1)
+        for ch in range(8):
+            if ch in AHEAD:
+                cashflow_pass(0, ch, 0, first=1)
+            else:
+                cashflow(0, ch)
         present_value(0, 0)
         round_piece("w2_10", nc.scalar.copy)
         last_rounded = kept([P, PACK, P, PACK], BF16, "last_rounded")

@@ -28,6 +28,7 @@ LIST_GROUP = 16
 HALF = 512
 CH = 128
 LINE = 4
+PAIR = 2
 OUT_TILES = N // P
 AHEAD = (0, 1, 2, 5, 6)
 BANKS = 8
@@ -170,9 +171,9 @@ def tile_list_scenario_cashflow_values_kernel(
                 nc.gpsimd.tensor_tensor(out=values[a, first][:, 0:CH, :], in0=parked[:], in1=woven[:], op=MULT)
                 return
             nc.vector.tensor_tensor(
-                out=values[a, first][:, i0 : i0 + CH, :].rearrange("p (c i) t -> p c t i", i=LINE),
-                in0=bank[:].rearrange("p t (c i) -> p c t i", i=LINE),
-                in1=disc[a, hf][:, :, j0 : j0 + CH].rearrange("p t (c i) -> p c t i", i=LINE),
+                out=values[a, first][:, i0 : i0 + CH, :].rearrange("p (c i) t -> p c t i", i=PAIR),
+                in0=bank[:].rearrange("p t (c i) -> p c t i", i=PAIR),
+                in1=disc[a, hf][:, :, j0 : j0 + CH].rearrange("p t (c i) -> p c t i", i=PAIR),
                 op=MULT,
             )
 

@@ -30,14 +30,21 @@ CH = 128
 LINE = 4
 PAIR = 2
 OUT_TILES = N // P
-AHEAD = (0, 1, 2, 5, 6)
+AHEAD = (0, 1, 2, 3, 6, 7)
+PARKED = ((0, 6), (0, 7), (1, 2), (1, 4))
+W1_CUT = 320
+LAST_CUT = 192
+CASH_BANKS = {0: (0, 1, 2, 3, 4, 5, 6, 7), 1: (6, 7, 2, 3, 4, 6, 2, 7)}
 BANKS = 8
 DISCOUNT_BANKS = 3
 
 W2_PIECES = {"w2_00": (0, 0), "w2_01": (1, 0), "w2_10": (0, 1), "w2_11": (1, 1)}
 PIECES = ["w1_0", "w1_1", *W2_PIECES]
 
-RUNS = {0: [(0, 4), (4, 6), (6, 7), (7, 8)], 1: [(0, 2), (2, 4), (4, 6), (6, 7), (7, 8)]}
+RUNS = {0: [(0, 2), (2, 4), (4, 6), (6, 7), (7, 8)], 1: [(0, 2), (2, 3), (3, 4), (4, 5), (5, 6), (6, 7), (7, 8)]}
+VALUES_AT = {(0, 4): 0, (0, 7): 2048}
+VALUES_ON = {(0, 6): "cash_words0", (1, 2): "values10", (1, 4): "values10"}
+CODES_AT = {(0, 1): 4096, (0, 3): 5120}
 
 
 def tile_list_scenario_cashflow_values_kernel(
@@ -47,10 +54,14 @@ def tile_list_scenario_cashflow_values_kernel(
     with ExitStack() as ctx:
         keep = ctx.enter_context(tc.tile_pool(name="keep", bufs=1))
         ring = ctx.enter_context(tc.tile_pool(name="ring", bufs=3))
+        shared = ctx.enter_context(tc.tile_pool(name="shared", bufs=1))
         psum = ctx.enter_context(tc.psum_pool(name="psum", bufs=1))
 
         def kept(shape, dtype, name):
-            return keep.tile(shape, dtype, name=name, align_bytes=64)
+            return keep.tile(shape, dtype, name=name, align_bytes=256)
+
+        def placed(shape, dtype, name, offset):
+            return shared.tile(shape, dtype, name=name, align_bytes=256, offset=offset)
 
         idx = kept([P, S // LIST_GROUP], U16, "idx")
         idx2 = kept([P, S // LIST_GROUP], U16, "idx2")
@@ -68,14 +79,17 @@ def tile_list_scenario_cashflow_values_kernel(
         planes = [kept([P, S // I32_BYTES], I32, "planes0"), kept([P, 2 * S // I32_BYTES], I32, "planes1")]
 
         raw_w1 = kept([P, PACK, H], F32, "raw_w1")
-        raw = {name: kept([P, PACK, KP], F32, "raw_" + name) for name in W2_PIECES}
+        raw = {name: kept([P, PACK, KP], F32, "raw_" + name) for name in ("w2_10",)}
+        raw["w2_00"] = placed([P, PACK, KP], F32, "raw_w2_00", 12288)
+        raw["w2_01"] = placed([P, PACK, KP], F32, "raw_w2_01", 20480)
+        raw["w2_11"] = placed([P, PACK, KP], F32, "raw_w2_11", 4096)
         raw["w1_0"], raw["w1_1"] = raw_w1[:, :, 0:KP], raw_w1[:, :, KP:H]
         w_codes = {name: kept([P, KP], U32, "codes_" + name) for name in PIECES}
         w_scales = {name: kept([P, KP], U8, "scales_" + name) for name in PIECES}
         disc = {(a, hf): kept([P, PACK, HALF], F32, f"disc{a}{hf}") for a in range(2) for hf in range(2)}
-        h_codes = {(a, hf): kept([P, HALF], U32, f"h_codes{a}{hf}") for a, hf in ((0, 0), (1, 0), (1, 1))}
-        h_scales = {(a, hf): kept([P, HALF], U8, f"h_scales{a}{hf}") for a in range(2) for hf in range(2)}
-        rounded, values, cash_bank, out_bank = {}, {}, {}, {}
+        h_codes = {}
+        h_scales = {(a, pr): kept([P, 2 * CH], U8, f"h_scales{a}{pr}") for a in range(2) for pr in range(4)}
+        rounded, values, cash_bank, out_bank, woven, parked = {}, {}, {}, {}, {}, {}
 
         nc.gpsimd.memset(curve_scales[:], 0)
         nc.vector.memset(cash_scales[:], 0)
@@ -83,8 +97,8 @@ def tile_list_scenario_cashflow_values_kernel(
         nc.vector.memset(planes[0][:], 0)
         nc.vector.memset(shift_scales[:], 0)
 
-        def load_words(tile, words):
-            nc.sync.dma_start(out=tile[:], in_=words.rearrange("p t i -> p (t i)").bitcast(I32))
+        def load_words(tile, words, t0, t1):
+            nc.sync.dma_start(out=tile[:, t0:t1], in_=words[:, t0:t1, :].rearrange("p t i -> p (t i)").bitcast(I32))
 
         def load_w2(name, c0=0, c1=KP):
             g, a = W2_PIECES[name]
@@ -104,7 +118,7 @@ def tile_list_scenario_cashflow_values_kernel(
 
         def round_piece(name, copy, cuts=(0, KP), grouped=None):
             if grouped is None:
-                grouped = ring.tile([P, PACK, P, PACK], BF16, name="grouped", align_bytes=64)
+                grouped = ring.tile([P, PACK, P, PACK], BF16, name="grouped", align_bytes=256)
             for c0, c1 in zip(cuts[:-1], cuts[1:]):
                 copy(
                     out=grouped[:, :, c0 // PACK : c1 // PACK, :].rearrange("p t m j -> p m j t"),
@@ -121,11 +135,11 @@ def tile_list_scenario_cashflow_values_kernel(
                     in_=rounded[name][:, t0:t1, :, :].rearrange("p t m j -> p (t m j)"),
                 )
 
-        def discount(a, hf):
+        def discount(a, hf, turn):
             name = f"w1_{a}"
             cols = slice(hf * HALF, (hf + 1) * HALF)
             for t in range(PACK):
-                bank = psum.tile([P, HALF], F32, name=f"bank{BANKS - 1 - (15 - (2 * a + hf) * PACK - t) % DISCOUNT_BANKS}")
+                bank = psum.tile([P, HALF], F32, name=f"bank{BANKS - 1 - (15 - turn * PACK - t) % DISCOUNT_BANKS}")
                 nc.tensor.matmul_mx(
                     out=bank[:],
                     lhsT=w_codes[name][:, t * P : (t + 1) * P].bitcast(FP8X4),
@@ -140,7 +154,7 @@ def tile_list_scenario_cashflow_values_kernel(
         def cashflow_pass(a, ch, g, t0=0, t1=PACK, first=0):
             cols = slice(ch * CH, (ch + 1) * CH)
             if (g, t0) == (first, 0):
-                cash_bank[a, ch] = psum.tile([P, PACK, CH], F32, name=f"bank{ch if a == 0 else 4 + ch % 4}")
+                cash_bank[a, ch] = psum.tile([P, PACK, CH], F32, name=f"bank{CASH_BANKS[a][ch]}")
             name = f"w2_{a}{g}"
             for t in range(t0, t1):
                 nc.tensor.matmul_mx(
@@ -157,32 +171,51 @@ def tile_list_scenario_cashflow_values_kernel(
             for g in range(2):
                 cashflow_pass(a, ch, g)
 
+        def weave(a, ch):
+            hf, j0 = divmod(ch * CH, HALF)
+            woven[a, ch] = placed([P, CH, PACK], F32, f"woven{a}{ch}", 12288 + 2048 * PARKED.index((a, ch)))
+            nc.vector.tensor_copy(
+                out=woven[a, ch][:].rearrange("p (c i) t -> p c t i", i=LINE),
+                in_=disc[a, hf][:, :, j0 : j0 + CH].rearrange("p t (c i) -> p c t i", i=LINE),
+            )
+
+        def park(a, ch):
+            parked[a, ch] = placed([P, CH, PACK], F32, f"parked{a}{ch}", 20480 + 2048 * PARKED.index((a, ch)))
+            nc.scalar.copy(out=parked[a, ch][:], in_=cash_bank[a, ch][:].rearrange("p t j -> p j t"))
+
         def present_value(a, ch):
-            bank = cash_bank[a, ch]
             hf, j0 = divmod(ch * CH, HALF)
             first, end = [run for run in RUNS[a] if run[0] <= ch < run[1]][0]
             if ch == first:
-                name = {(0, 7): "last_rounded", (1, 6): "values14"}.get((a, first), f"values{a}{first}")
-                values[a, first] = kept([P, (end - first) * CH, PACK], BF16, name)
+                shape = [P, (end - first) * CH, PACK]
+                if (a, first) in VALUES_AT:
+                    values[a, first] = placed(shape, BF16, f"values{a}{first}", VALUES_AT[a, first])
+                else:
+                    values[a, first] = kept(shape, BF16, VALUES_ON.get((a, first), f"values{a}{first}"))
             i0 = (ch - first) * CH
-            if (a, ch) == (0, 0):
-                parked = kept([P, CH, PACK], F32, "parked")
-                nc.scalar.copy(out=parked[:], in_=bank[:].rearrange("p t j -> p j t"))
-                nc.gpsimd.tensor_tensor(out=values[a, first][:, 0:CH, :], in0=parked[:], in1=woven[:], op=MULT)
+            if (a, ch) in parked:
+                nc.gpsimd.tensor_tensor(
+                    out=values[a, first][:, i0 : i0 + CH, :], in0=parked[a, ch][:], in1=woven[a, ch][:], op=MULT
+                )
                 return
             nc.vector.tensor_tensor(
                 out=values[a, first][:, i0 : i0 + CH, :].rearrange("p (c i) t -> p c t i", i=PAIR),
-                in0=bank[:].rearrange("p t (c i) -> p c t i", i=PAIR),
+                in0=cash_bank[a, ch][:].rearrange("p t (c i) -> p c t i", i=PAIR),
                 in1=disc[a, hf][:, :, j0 : j0 + CH].rearrange("p t (c i) -> p c t i", i=PAIR),
                 op=MULT,
             )
 
         def quantize_run(a, first):
-            hf, j0 = divmod(first * CH, HALF)
+            pr, j0 = divmod(first * CH, 2 * CH)
+            if (a, pr) not in h_codes:
+                if (a, pr) in CODES_AT:
+                    h_codes[a, pr] = placed([P, 2 * CH], U32, f"h_codes{a}{pr}", CODES_AT[a, pr])
+                else:
+                    h_codes[a, pr] = kept([P, 2 * CH], U32, f"h_codes{a}{pr}")
             j1 = j0 + values[a, first].shape[1]
             nc.vector.quantize_mx(
-                out=h_codes[a, hf][:, j0:j1].bitcast(FP8X4),
-                scales=h_scales[a, hf][:, j0:j1],
+                out=h_codes[a, pr][:, j0:j1].bitcast(FP8X4),
+                scales=h_scales[a, pr][:, j0:j1],
                 in_=values[a, first][:].rearrange("p j t -> p (j t)"),
             )
 
@@ -190,14 +223,14 @@ def tile_list_scenario_cashflow_values_kernel(
             width = (ch1 - ch0) * CH
             if a == 0:
                 out_bank[u0, ch0] = psum.tile([P, u1 - u0, width], F32, name=f"bank{bank}")
-            hf, j0 = divmod(ch0 * CH, HALF)
+            pr = ch0 // 2
             for u in range(u0, u1):
                 nc.tensor.matmul_mx(
                     out=out_bank[u0, ch0][:, u - u0, :],
                     lhsT=shift_words[a][:].bitcast(U8)[:, 2 * P * u : 2 * P * (u + 1)].bitcast(FP4X4),
                     lhsT_scale=shift_scales[:, a, :].bitcast(U8)[:, P * u : P * (u + 1)],
-                    rhs=h_codes[a, hf][:, j0 : j0 + width].bitcast(FP8X4),
-                    rhs_scale=h_scales[a, hf][:, j0 : j0 + width],
+                    rhs=h_codes[a, pr][:].bitcast(FP8X4),
+                    rhs_scale=h_scales[a, pr][:],
                     start=(a == 0 and u == u0),
                     stop=(a == 1 and u == u1 - 1),
                 )
@@ -219,9 +252,9 @@ def tile_list_scenario_cashflow_values_kernel(
                     )
             store(result[:], u0, u1, ch0 * CH, ch1 * CH)
 
-        def open_pair(ch, first_bank):
+        def open_pair(ch, banks):
             for i in range(2):
-                scenario_pass(0, first_bank + i, 2 * i, 2 * i + 2, ch, ch + 2)
+                scenario_pass(0, banks[i], 2 * i, 2 * i + 2, ch, ch + 2)
 
         def close_pair(ch):
             for i in range(2):
@@ -232,30 +265,32 @@ def tile_list_scenario_cashflow_values_kernel(
         def store(result, u0, u1, j0, j1):
             nc.sync.dma_start(out=out[u0 * P : u1 * P, j0:j1].rearrange("(u p) j -> p u j", p=P), in_=result)
 
-        load_words(curve_words, tab_words[0])
+        load_words(curve_words, tab_words[0], 0, T // 2)
         nc.sync.dma_start(idx2[:], offs2)
         nc.sync.dma_start(out=cash_scales[0:P:4, :], in_=tab2_scales.bitcast(I32).rearrange("g q t -> (g q) t"))
         nc.sync.dma_start(out=curve_scales[4 * BLOCKS : P : 4, :], in_=tab_scales[0].bitcast(I32))
         nc.sync.dma_start(idx[:], offs)
+        load_words(curve_words, tab_words[0], T // 2, T)
         nc.sync.dma_start(out=raw_w1[:], in_=w1.rearrange("(p j) c -> p j c", j=PACK))
         nc.sync.dma_start(out=bias[:, :, 0:PACK], in_=b1.rearrange("(a p t) -> p a t", a=2, t=PACK))
-        load_words(cash_words[1], tab2_words[1])
+        load_words(cash_words[1], tab2_words[1], 0, T2 // 2)
 
         gather(rows[:, S:], cash_scales[:].bitcast(U8), idx2, 0, S)
         gather(rows[:, 0:S], curve_scales[:].bitcast(U8), idx, 0, S)
         gather(v_words, curve_words[:].bitcast(U32), idx, 0, S)
 
         place_scales(1)
+        load_words(cash_words[1], tab2_words[1], T2 // 2, T2)
+        place_scales(0)
         load_w2("w2_01")
+        load_w2("w2_00")
+        load_words(cash_words[0], tab2_words[0], 0, T2)
+        load_w2("w2_10")
         for s in range(SCALE_ROWS):
             nc.sync.dma_start(
                 out=shift_scales[s:P:QUADRANT, :, :],
                 in_=w4_scales.bitcast(I32)[:, s:BLOCKS:SCALE_ROWS, :].rearrange("a q n -> q a n"),
             )
-        load_w2("w2_00")
-        load_words(cash_words[0], tab2_words[0])
-        place_scales(0)
-        load_w2("w2_10")
         nc.sync.dma_start(out=shift_words[0][:], in_=w4_words[0].bitcast(I32))
         load_w2("w2_11", 0, KP // 2)
         load_w2("w2_11", KP // 2, KP)
@@ -263,82 +298,85 @@ def tile_list_scenario_cashflow_values_kernel(
         with nc.allow_non_contiguous_dma(reason="one rate to a partition and output tile"):
             nc.sync.dma_start(out=rate[:], in_=fx.rearrange("(u p) -> p u", p=P))
 
-        for a in range(2):
-            round_piece(f"w1_{a}", nc.scalar.copy)
-            quantize_piece(f"w1_{a}")
-        for a in range(2):
-            for hf in range(2):
-                discount(a, hf)
+        round_piece("w1_0", nc.scalar.copy)
+        both = ring.tile([P, PACK, P, PACK], BF16, name="grouped", align_bytes=256)
+        round_piece("w1_1", nc.vector.tensor_copy, (0, W1_CUT), both)
+        quantize_piece("w1_0")
+        round_piece("w1_1", nc.scalar.copy, (W1_CUT, KP), both)
+        quantize_piece("w1_1")
+        for turn, (a, hf) in enumerate(((0, 1), (1, 0), (1, 1), (0, 0))):
+            discount(a, hf, turn)
 
         gather(v2_words[1], cash_words[1][:].bitcast(U32), idx2, 0, S)
         round_piece("w2_01", nc.vector.tensor_copy)
         quantize_piece("w2_01")
         round_piece("w2_00", nc.vector.tensor_copy)
         quantize_piece("w2_00")
-        woven = kept([P, CH, PACK], F32, "woven")
-        nc.vector.tensor_copy(
-            out=woven[:].rearrange("p (c i) t -> p c t i", i=LINE),
-            in_=disc[0, 0][:, :, 0:CH].rearrange("p t (c i) -> p c t i", i=LINE),
-        )
-        for hf in range(2):
-            gather(v2_words[0], cash_words[0][:].bitcast(U32), idx2, hf * HALF, (hf + 1) * HALF)
+        for a, ch in PARKED:
+            weave(a, ch)
+        for pr in (3, 0, 1, 2):
+            gather(v2_words[0], cash_words[0][:].bitcast(U32), idx2, pr * 2 * CH, (pr + 1) * 2 * CH)
 
         for ch in AHEAD:
             cashflow_pass(0, ch, 1, first=1)
-        for ch in range(8):
-            if ch in AHEAD:
-                cashflow_pass(0, ch, 0, first=1)
-            else:
-                cashflow(0, ch)
-        present_value(0, 0)
+        for ch in (6, 7, 0, 1, 2, 3):
+            cashflow_pass(0, ch, 0, first=1)
+        cashflow(0, 4)
+        cashflow(0, 5)
+        park(0, 6)
+        park(0, 7)
+        present_value(0, 6)
         round_piece("w2_10", nc.scalar.copy)
-        last_rounded = kept([P, PACK, P, PACK], BF16, "last_rounded")
-        round_piece("w2_11", nc.scalar.copy, (KP // 4, KP // 2, KP), last_rounded)
-        for ch in range(1, 5):
+        last_rounded = placed([P, PACK, P, PACK], BF16, "last_rounded", 0)
+        round_piece("w2_11", nc.scalar.copy, (LAST_CUT, KP // 2, KP), last_rounded)
+        for ch in range(3):
             present_value(0, ch)
         quantize_run(0, 0)
-        open_pair(0, 0)
-        open_pair(2, 2)
+        open_pair(0, (0, 1))
+        present_value(0, 3)
         quantize_piece("w2_10")
-        cashflow_pass(1, 0, 0)
-        round_piece("w2_11", nc.vector.tensor_copy, (0, KP // 4), last_rounded)
-        for ch in range(5, 7):
-            present_value(0, ch)
-            cashflow_pass(1, ch - 4, 0)
-
+        for ch in range(4):
+            cashflow_pass(1, ch, 0)
+        round_piece("w2_11", nc.vector.tensor_copy, (0, LAST_CUT), last_rounded)
         quantize_piece("w2_11", calls=2)
         for t0 in (0, 2):
             for ch in range(2):
                 cashflow_pass(1, ch, 1, t0, t0 + 2)
         cashflow_pass(1, 2, 1)
-        present_value(0, 7)
-        cashflow(1, 3)
+        cashflow_pass(1, 3, 1)
 
-        present_value(1, 0)
+        park(1, 2)
+
+        quantize_run(0, 2)
+        present_value(0, 7)
+        present_value(0, 4)
         cashflow(1, 4)
+        park(1, 4)
+        present_value(1, 0)
+        cashflow(1, 5)
         present_value(1, 1)
-        cashflow_pass(1, 5, 0)
-        h_codes[0, 1] = kept([P, HALF], U32, "raw_w2_11")
-        quantize_run(0, 4)
+        quantize_run(0, 6)
+        quantize_run(0, 7)
         quantize_run(1, 0)
         close_pair(0)
-        cashflow_pass(1, 5, 1)
-        present_value(1, 2)
         cashflow(1, 6)
+        present_value(1, 2)
+        present_value(0, 5)
+        open_pair(2, (4, 5))
         present_value(1, 3)
-        cashflow_pass(1, 7, 0)
-        quantize_run(0, 6)
+        quantize_run(0, 4)
+        quantize_run(1, 3)
         quantize_run(1, 2)
         close_pair(2)
-        open_pair(4, 0)
-        cashflow_pass(1, 7, 1)
+        cashflow(1, 7)
         present_value(1, 4)
+        open_pair(4, (0, 1))
         present_value(1, 5)
-        quantize_run(0, 7)
+        present_value(1, 6)
+        quantize_run(1, 5)
         quantize_run(1, 4)
         close_pair(4)
-        present_value(1, 6)
-        for u, bank in enumerate((4, 5, 2, 6)):
+        for u, bank in enumerate((3, 6, 2, 4)):
             scenario_pass(0, bank, u, u + 1, 6, 8)
         present_value(1, 7)
         quantize_run(1, 6)

@@ -91,8 +91,8 @@ def tile_list_scenario_cashflow_values_kernel(
         h_scales = {(a, pr): kept([P, 2 * CH], U8, f"h_scales{a}{pr}") for a in range(2) for pr in range(4)}
         rounded, values, cash_bank, out_bank, woven, parked = {}, {}, {}, {}, {}, {}
 
-        nc.gpsimd.memset(curve_scales[:], 0)
         nc.vector.memset(cash_scales[:], 0)
+        nc.vector.memset(curve_scales[:], 0)
         nc.vector.memset(planes[1][:], 0)
         nc.vector.memset(planes[0][:], 0)
         nc.vector.memset(shift_scales[:], 0)
@@ -265,24 +265,24 @@ def tile_list_scenario_cashflow_values_kernel(
         def store(result, u0, u1, j0, j1):
             nc.sync.dma_start(out=out[u0 * P : u1 * P, j0:j1].rearrange("(u p) j -> p u j", p=P), in_=result)
 
-        load_words(curve_words, tab_words[0], 0, T // 2)
+        load_words(curve_words, tab_words[0], 0, 3 * T // 4)
         nc.sync.dma_start(idx2[:], offs2)
+        nc.sync.dma_start(idx[:], offs)
         nc.sync.dma_start(out=cash_scales[0:P:4, :], in_=tab2_scales.bitcast(I32).rearrange("g q t -> (g q) t"))
         nc.sync.dma_start(out=curve_scales[4 * BLOCKS : P : 4, :], in_=tab_scales[0].bitcast(I32))
-        nc.sync.dma_start(idx[:], offs)
-        load_words(curve_words, tab_words[0], T // 2, T)
+        load_words(curve_words, tab_words[0], 3 * T // 4, T)
         nc.sync.dma_start(out=raw_w1[:], in_=w1.rearrange("(p j) c -> p j c", j=PACK))
         nc.sync.dma_start(out=bias[:, :, 0:PACK], in_=b1.rearrange("(a p t) -> p a t", a=2, t=PACK))
-        load_words(cash_words[1], tab2_words[1], 0, T2 // 2)
+        load_words(cash_words[1], tab2_words[1], 0, 5 * T2 // 8)
 
         gather(rows[:, S:], cash_scales[:].bitcast(U8), idx2, 0, S)
         gather(rows[:, 0:S], curve_scales[:].bitcast(U8), idx, 0, S)
         gather(v_words, curve_words[:].bitcast(U32), idx, 0, S)
 
         place_scales(1)
-        load_words(cash_words[1], tab2_words[1], T2 // 2, T2)
-        place_scales(0)
+        load_words(cash_words[1], tab2_words[1], 5 * T2 // 8, T2)
         load_w2("w2_01")
+        place_scales(0)
         load_w2("w2_00")
         load_words(cash_words[0], tab2_words[0], 0, T2)
         load_w2("w2_10")

@@ -31,20 +31,20 @@ LINE = 4
 PAIR = 2
 OUT_TILES = N // P
 AHEAD = (0, 1, 2, 3, 6, 7)
-PARKED = ((0, 6), (0, 7), (1, 2), (1, 4))
+PARKED = ((0, 6), (0, 7), (1, 2))
 W1_CUT = 320
 LAST_CUT = 192
-CASH_BANKS = {0: (0, 1, 2, 3, 4, 5, 6, 7), 1: (6, 7, 2, 3, 4, 6, 2, 7)}
+CASH_BANKS = {0: (0, 1, 2, 3, 4, 5, 6, 7), 1: (6, 7, 2, 3, 4, 6, 5, 4)}
 BANKS = 8
 DISCOUNT_BANKS = 3
 
 W2_PIECES = {"w2_00": (0, 0), "w2_01": (1, 0), "w2_10": (0, 1), "w2_11": (1, 1)}
 PIECES = ["w1_0", "w1_1", *W2_PIECES]
 
-RUNS = {0: [(0, 2), (2, 4), (4, 6), (6, 7), (7, 8)], 1: [(0, 2), (2, 3), (3, 4), (4, 5), (5, 6), (6, 7), (7, 8)]}
+RUNS = {0: [(0, 2), (2, 4), (4, 6), (6, 7), (7, 8)], 1: [(0, 2), (2, 3), (3, 4), (4, 6), (6, 7), (7, 8)]}
 VALUES_AT = {(0, 4): 0, (0, 7): 2048}
-VALUES_ON = {(0, 6): "cash_words0", (1, 2): "values10", (1, 4): "values10"}
-CODES_AT = {(0, 1): 4096, (0, 3): 5120}
+VALUES_ON = {(0, 6): "cash_words0", (1, 2): "values10"}
+CODES_AT = {(0, 1): 4096, (0, 3): 22528}
 
 
 def tile_list_scenario_cashflow_values_kernel(
@@ -104,6 +104,13 @@ def tile_list_scenario_cashflow_values_kernel(
             g, a = W2_PIECES[name]
             src = w2[g * KP : (g + 1) * KP, a * KP + c0 : a * KP + c1]
             nc.sync.dma_start(out=raw[name][:, :, c0:c1], in_=src.rearrange("(p j) c -> p j c", j=PACK))
+
+        def load_shift_scales(s0, s1):
+            for s in range(s0, s1):
+                nc.sync.dma_start(
+                    out=shift_scales[s:P:QUADRANT, :, :],
+                    in_=w4_scales.bitcast(I32)[:, s:BLOCKS:SCALE_ROWS, :].rearrange("a q n -> q a n"),
+                )
 
         def place_scales(g):
             c0 = 0 if g == 1 else S // I32_BYTES
@@ -285,12 +292,9 @@ def tile_list_scenario_cashflow_values_kernel(
         place_scales(0)
         load_w2("w2_00")
         load_words(cash_words[0], tab2_words[0], 0, T2)
+        load_shift_scales(0, 2)
         load_w2("w2_10")
-        for s in range(SCALE_ROWS):
-            nc.sync.dma_start(
-                out=shift_scales[s:P:QUADRANT, :, :],
-                in_=w4_scales.bitcast(I32)[:, s:BLOCKS:SCALE_ROWS, :].rearrange("a q n -> q a n"),
-            )
+        load_shift_scales(2, SCALE_ROWS)
         nc.sync.dma_start(out=shift_words[0][:], in_=w4_words[0].bitcast(I32))
         load_w2("w2_11", 0, KP // 2)
         load_w2("w2_11", KP // 2, KP)
@@ -334,9 +338,12 @@ def tile_list_scenario_cashflow_values_kernel(
         quantize_run(0, 0)
         open_pair(0, (0, 1))
         present_value(0, 3)
-        quantize_piece("w2_10")
-        for ch in range(4):
-            cashflow_pass(1, ch, 0)
+        quantize_piece("w2_10", calls=2)
+        for t0 in (0, 2):
+            for ch in range(2):
+                cashflow_pass(1, ch, 0, t0, t0 + 2)
+        cashflow_pass(1, 2, 0)
+        cashflow_pass(1, 3, 0)
         round_piece("w2_11", nc.vector.tensor_copy, (0, LAST_CUT), last_rounded)
         quantize_piece("w2_11", calls=2)
         for t0 in (0, 2):
@@ -351,7 +358,6 @@ def tile_list_scenario_cashflow_values_kernel(
         present_value(0, 7)
         present_value(0, 4)
         cashflow(1, 4)
-        park(1, 4)
         present_value(1, 0)
         cashflow(1, 5)
         present_value(1, 1)
@@ -359,24 +365,23 @@ def tile_list_scenario_cashflow_values_kernel(
         quantize_run(0, 7)
         quantize_run(1, 0)
         close_pair(0)
-        cashflow(1, 6)
         present_value(1, 2)
         present_value(0, 5)
-        open_pair(2, (4, 5))
+        cashflow(1, 6)
         present_value(1, 3)
+        open_pair(2, (2, 3))
+        present_value(1, 4)
+        cashflow(1, 7)
         quantize_run(0, 4)
         quantize_run(1, 3)
         quantize_run(1, 2)
         close_pair(2)
-        cashflow(1, 7)
-        present_value(1, 4)
-        open_pair(4, (0, 1))
+        open_pair(4, (7, 0))
         present_value(1, 5)
         present_value(1, 6)
-        quantize_run(1, 5)
         quantize_run(1, 4)
         close_pair(4)
-        for u, bank in enumerate((3, 6, 2, 4)):
+        for u, bank in enumerate((1, 6, 5, 2)):
             scenario_pass(0, bank, u, u + 1, 6, 8)
         present_value(1, 7)
         quantize_run(1, 6)

@@ -31,19 +31,19 @@ LINE = 4
 PAIR = 2
 OUT_TILES = N // P
 AHEAD = (0, 1, 2, 3, 6, 7)
-PARKED = ((0, 6), (0, 7), (1, 2))
+PARKED = ((0, 6), (0, 7), (1, 4))
 W1_CUT = 320
 LAST_CUT = 192
-CASH_BANKS = {0: (0, 1, 2, 3, 4, 5, 6, 7), 1: (6, 7, 2, 3, 4, 6, 5, 4)}
+CASH_BANKS = {0: (0, 1, 2, 3, 4, 5, 6, 7), 1: (6, 7, 2, 3, 4, 6, 3, 0)}
 BANKS = 8
 DISCOUNT_BANKS = 3
 
 W2_PIECES = {"w2_00": (0, 0), "w2_01": (1, 0), "w2_10": (0, 1), "w2_11": (1, 1)}
 PIECES = ["w1_0", "w1_1", *W2_PIECES]
 
-RUNS = {0: [(0, 2), (2, 4), (4, 6), (6, 7), (7, 8)], 1: [(0, 2), (2, 3), (3, 4), (4, 6), (6, 7), (7, 8)]}
+RUNS = {0: [(0, 2), (2, 4), (4, 6), (6, 7), (7, 8)], 1: [(0, 2), (2, 4), (4, 5), (5, 6), (6, 7), (7, 8)]}
 VALUES_AT = {(0, 4): 0, (0, 7): 2048}
-VALUES_ON = {(0, 6): "cash_words0", (1, 2): "values10"}
+VALUES_ON = {(0, 6): "cash_words0", (1, 4): "values10"}
 CODES_AT = {(0, 1): 4096, (0, 3): 22528}
 
 
@@ -352,12 +352,12 @@ def tile_list_scenario_cashflow_values_kernel(
         cashflow_pass(1, 2, 1)
         cashflow_pass(1, 3, 1)
 
-        park(1, 2)
 
         quantize_run(0, 2)
         present_value(0, 7)
         present_value(0, 4)
         cashflow(1, 4)
+        park(1, 4)
         present_value(1, 0)
         cashflow(1, 5)
         present_value(1, 1)
@@ -365,23 +365,23 @@ def tile_list_scenario_cashflow_values_kernel(
         quantize_run(0, 7)
         quantize_run(1, 0)
         close_pair(0)
-        present_value(1, 2)
-        present_value(0, 5)
-        cashflow(1, 6)
-        present_value(1, 3)
-        open_pair(2, (2, 3))
         present_value(1, 4)
-        cashflow(1, 7)
-        quantize_run(0, 4)
-        quantize_run(1, 3)
+        present_value(1, 2)
+        open_pair(2, (7, 2))
+        present_value(1, 3)
+        cashflow(1, 6)
+        present_value(0, 5)
         quantize_run(1, 2)
         close_pair(2)
-        open_pair(4, (7, 0))
+        cashflow(1, 7)
         present_value(1, 5)
-        present_value(1, 6)
+        quantize_run(0, 4)
+        open_pair(4, (4, 5))
         quantize_run(1, 4)
+        quantize_run(1, 5)
         close_pair(4)
-        for u, bank in enumerate((1, 6, 5, 2)):
+        present_value(1, 6)
+        for u, bank in enumerate((1, 6, 7, 3)):
             scenario_pass(0, bank, u, u + 1, 6, 8)
         present_value(1, 7)
         quantize_run(1, 6)

@@ -1,6 +1,7 @@
 from contextlib import ExitStack
 
 import concourse.mybir as mybir
+from concourse.masks import make_identity
 
 K, M, H, N, T, T2, S = 512, 1024, 1024, 512, 2048, 4096, 1024
 FLOPS = 2 * S * (K * H + M * H + H * N)
@@ -71,7 +72,7 @@ def tile_list_scenario_cashflow_values_kernel(
         cash_scales = kept([P, T2 // I32_BYTES], I32, "cash_scales")
         shift_words = [kept([P, 2 * N // I32_BYTES], I32, f"shift_words{a}") for a in range(2)]
         shift_scales = kept([P, 2, N // I32_BYTES], I32, "shift_scales")
-        bias = kept([P, 2, 2 * PACK], F32, "bias")
+        bias = kept([P, 2, PACK], F32, "bias")
         rate = kept([P, OUT_TILES], F32, "rate")
         v_words = kept([P, S], U32, "v_words")
         v2_words = [kept([P, S], U32, f"v2_words{g}") for g in range(2)]
@@ -96,6 +97,11 @@ def tile_list_scenario_cashflow_values_kernel(
         nc.vector.memset(planes[1][:], 0)
         nc.vector.memset(planes[0][:], 0)
         nc.vector.memset(shift_scales[:], 0)
+        bias_rows = kept([P, KP], F32, "values10")
+        identity = kept([P, P], F32, "values12")
+        nc.vector.memset(bias_rows[:], 0.0)
+        nc.vector.memset(identity[:], 0.0)
+        make_identity(nc, identity[:], nomemset=True)
 
         def load_words(tile, words, t0, t1):
             nc.sync.dma_start(out=tile[:, t0:t1], in_=words[:, t0:t1, :].rearrange("p t i -> p (t i)").bitcast(I32))
@@ -279,7 +285,7 @@ def tile_list_scenario_cashflow_values_kernel(
         nc.sync.dma_start(out=curve_scales[4 * BLOCKS : P : 4, :], in_=tab_scales[0].bitcast(I32))
         load_words(curve_words, tab_words[0], 3 * T // 4, T)
         nc.sync.dma_start(out=raw_w1[:], in_=w1.rearrange("(p j) c -> p j c", j=PACK))
-        nc.sync.dma_start(out=bias[:, :, 0:PACK], in_=b1.rearrange("(a p t) -> p a t", a=2, t=PACK))
+        nc.sync.dma_start(out=bias_rows[0:2, :], in_=b1.rearrange("(a c) -> a c", a=2))
         load_words(cash_words[1], tab2_words[1], 0, 5 * T2 // 8)
 
         gather(rows[:, S:], cash_scales[:].bitcast(U8), idx2, 0, S)
@@ -302,7 +308,11 @@ def tile_list_scenario_cashflow_values_kernel(
         with nc.allow_non_contiguous_dma(reason="one rate to a partition and output tile"):
             nc.sync.dma_start(out=rate[:], in_=fx.rearrange("(u p) -> p u", p=P))
 
+        turned = psum.tile([P, PACK, P], F32, name="bank0")
+        for t in range(PACK):
+            nc.tensor.transpose(turned[:, t, :], bias_rows[:, t:KP:PACK], identity[:])
         round_piece("w1_0", nc.scalar.copy)
+        nc.scalar.copy(out=bias[:], in_=turned[:, :, 0:2].rearrange("p t a -> p a t"))
         both = ring.tile([P, PACK, P, PACK], BF16, name="grouped", align_bytes=256)
         round_piece("w1_1", nc.vector.tensor_copy, (0, W1_CUT), both)
         quantize_piece("w1_0")

@@ -35,7 +35,7 @@ AHEAD = (0, 1, 2, 3, 6, 7)
 PARKED = ((0, 6), (0, 7), (1, 4))
 W1_CUT = 320
 LAST_CUT = 192
-CASH_BANKS = {0: (0, 1, 2, 3, 4, 5, 6, 7), 1: (6, 7, 2, 3, 4, 6, 3, 0)}
+CASH_BANKS = {0: (0, 1, 2, 3, 4, 5, 6, 7), 1: (6, 7, 2, 4, 3, 6, 4, 0)}
 BANKS = 8
 DISCOUNT_BANKS = 3
 
@@ -43,8 +43,7 @@ W2_PIECES = {"w2_00": (0, 0), "w2_01": (1, 0), "w2_10": (0, 1), "w2_11": (1, 1)}
 PIECES = ["w1_0", "w1_1", *W2_PIECES]
 
 RUNS = {0: [(0, 2), (2, 4), (4, 6), (6, 7), (7, 8)], 1: [(0, 2), (2, 4), (4, 5), (5, 6), (6, 7), (7, 8)]}
-VALUES_AT = {(0, 4): 0, (0, 7): 2048}
-VALUES_ON = {(0, 6): "cash_words0", (1, 4): "values10"}
+VALUES_AT = {(0, 4): 0, (0, 7): 2048, (1, 4): 2048}
 CODES_AT = {(0, 1): 4096, (0, 3): 22528}
 
 
@@ -204,7 +203,7 @@ def tile_list_scenario_cashflow_values_kernel(
                 if (a, first) in VALUES_AT:
                     values[a, first] = placed(shape, BF16, f"values{a}{first}", VALUES_AT[a, first])
                 else:
-                    values[a, first] = kept(shape, BF16, VALUES_ON.get((a, first), f"values{a}{first}"))
+                    values[a, first] = kept(shape, BF16, f"values{a}{first}")
             i0 = (ch - first) * CH
             if (a, ch) in parked:
                 nc.gpsimd.tensor_tensor(
@@ -328,8 +327,8 @@ def tile_list_scenario_cashflow_values_kernel(
         quantize_piece("w2_00")
         for a, ch in PARKED:
             weave(a, ch)
-        for pr in (3, 0, 1, 2):
-            gather(v2_words[0], cash_words[0][:].bitcast(U32), idx2, pr * 2 * CH, (pr + 1) * 2 * CH)
+        for ch0, ch1 in ((6, 8), (0, 2), (2, 6)):
+            gather(v2_words[0], cash_words[0][:].bitcast(U32), idx2, ch0 * CH, ch1 * CH)
 
         for ch in AHEAD:
             cashflow_pass(0, ch, 1, first=1)
@@ -353,21 +352,21 @@ def tile_list_scenario_cashflow_values_kernel(
             for ch in range(2):
                 cashflow_pass(1, ch, 0, t0, t0 + 2)
         cashflow_pass(1, 2, 0)
-        cashflow_pass(1, 3, 0)
+        cashflow_pass(1, 4, 0)
         round_piece("w2_11", nc.vector.tensor_copy, (0, LAST_CUT), last_rounded)
         quantize_piece("w2_11", calls=2)
         for t0 in (0, 2):
             for ch in range(2):
                 cashflow_pass(1, ch, 1, t0, t0 + 2)
+        cashflow_pass(1, 4, 1)
+        park(1, 4)
         cashflow_pass(1, 2, 1)
-        cashflow_pass(1, 3, 1)
 
 
         quantize_run(0, 2)
         present_value(0, 7)
         present_value(0, 4)
-        cashflow(1, 4)
-        park(1, 4)
+        cashflow(1, 3)
         present_value(1, 0)
         cashflow(1, 5)
         present_value(1, 1)
@@ -386,12 +385,12 @@ def tile_list_scenario_cashflow_values_kernel(
         cashflow(1, 7)
         present_value(1, 5)
         quantize_run(0, 4)
-        open_pair(4, (4, 5))
+        open_pair(4, (3, 5))
         quantize_run(1, 4)
         quantize_run(1, 5)
         close_pair(4)
         present_value(1, 6)
-        for u, bank in enumerate((1, 6, 7, 3)):
+        for u, bank in enumerate((1, 6, 7, 4)):
             scenario_pass(0, bank, u, u + 1, 6, 8)
         present_value(1, 7)
         quantize_run(1, 6)

@@ -35,7 +35,7 @@ AHEAD = (0, 1, 2, 3, 6, 7)
 PARKED = ((0, 6), (0, 7), (1, 4))
 W1_CUT = 320
 LAST_CUT = 192
-CASH_BANKS = {0: (0, 1, 2, 3, 4, 5, 6, 7), 1: (6, 7, 2, 4, 3, 6, 4, 0)}
+CASH_BANKS = {0: (0, 1, 2, 3, 4, 5, 6, 7), 1: (6, 7, 2, 4, 3, 6, 3, 4)}
 BANKS = 8
 DISCOUNT_BANKS = 3
 
@@ -374,23 +374,25 @@ def tile_list_scenario_cashflow_values_kernel(
         quantize_run(0, 7)
         quantize_run(1, 0)
         close_pair(0)
+        cashflow(1, 6)
         present_value(1, 4)
         present_value(1, 2)
         open_pair(2, (7, 2))
         present_value(1, 3)
-        cashflow(1, 6)
+        cashflow(1, 7)
         present_value(0, 5)
         quantize_run(1, 2)
         close_pair(2)
-        cashflow(1, 7)
         present_value(1, 5)
+        for u, bank in ((0, 1), (1, 6)):
+            scenario_pass(0, bank, u, u + 1, 6, 8)
         quantize_run(0, 4)
-        open_pair(4, (3, 5))
+        open_pair(4, (5, 0))
         quantize_run(1, 4)
         quantize_run(1, 5)
         close_pair(4)
         present_value(1, 6)
-        for u, bank in enumerate((1, 6, 7, 4)):
+        for u, bank in ((2, 7), (3, 3)):
             scenario_pass(0, bank, u, u + 1, 6, 8)
         present_value(1, 7)
         quantize_run(1, 6)

@@ -55,31 +55,38 @@ def tile_list_scenario_cashflow_values_kernel(
         keep = ctx.enter_context(tc.tile_pool(name="keep", bufs=1))
         ring = ctx.enter_context(tc.tile_pool(name="ring", bufs=3))
         shared = ctx.enter_context(tc.tile_pool(name="shared", bufs=1))
+        moved = ctx.enter_context(tc.tile_pool(name="moved", bufs=1))
         psum = ctx.enter_context(tc.psum_pool(name="psum", bufs=1))
 
         def kept(shape, dtype, name):
             return keep.tile(shape, dtype, name=name, align_bytes=256)
 
+        taken = []
+
+        def lined(shape, dtype, name, size):
+            taken.append(size)
+            return moved.tile(shape, dtype, name=name, align_bytes=1024, offset=1024 * (sum(taken) - size))
+
         def placed(shape, dtype, name, offset):
-            return shared.tile(shape, dtype, name=name, align_bytes=256, offset=offset)
+            return shared.tile(shape, dtype, name=name, align_bytes=1024, offset=offset)
 
         idx = kept([P, S // LIST_GROUP], U16, "idx")
         idx2 = kept([P, S // LIST_GROUP], U16, "idx2")
-        curve_words = kept([P, T], I32, "curve_words")
-        curve_scales = kept([P, T // I32_BYTES], I32, "curve_scales")
-        cash_words = [kept([P, T2], I32, f"cash_words{g}") for g in range(2)]
-        cash_scales = kept([P, T2 // I32_BYTES], I32, "cash_scales")
-        shift_words = [kept([P, 2 * N // I32_BYTES], I32, f"shift_words{a}") for a in range(2)]
-        shift_scales = kept([P, 2, N // I32_BYTES], I32, "shift_scales")
+        curve_words = lined([P, T], I32, "curve_words", 8)
+        curve_scales = lined([P, T // I32_BYTES], I32, "curve_scales", 2)
+        cash_words = [lined([P, T2], I32, f"cash_words{g}", 16) for g in range(2)]
+        cash_scales = lined([P, T2 // I32_BYTES], I32, "cash_scales", 4)
+        shift_words = [lined([P, 2 * N // I32_BYTES], I32, f"shift_words{a}", 1) for a in range(2)]
+        shift_scales = lined([P, 2, N // I32_BYTES], I32, "shift_scales", 1)
         bias = kept([P, 2, PACK], F32, "bias")
         rate = kept([P, OUT_TILES], F32, "rate")
         v_words = kept([P, S], U32, "v_words")
         v2_words = [kept([P, S], U32, f"v2_words{g}") for g in range(2)]
-        rows = kept([P, 2 * S], U8, "rows")
-        planes = [kept([P, S // I32_BYTES], I32, "planes0"), kept([P, 2 * S // I32_BYTES], I32, "planes1")]
+        rows = lined([P, 2 * S], U8, "rows", 2)
+        planes = [lined([P, S // I32_BYTES], I32, "planes0", 1), lined([P, 2 * S // I32_BYTES], I32, "planes1", 2)]
 
-        raw_w1 = kept([P, PACK, H], F32, "raw_w1")
-        raw = {name: kept([P, PACK, KP], F32, "raw_" + name) for name in ("w2_10",)}
+        raw_w1 = lined([P, PACK, H], F32, "raw_w1", 16)
+        raw = {name: lined([P, PACK, KP], F32, "raw_" + name, 8) for name in ("w2_10",)}
         raw["w2_00"] = placed([P, PACK, KP], F32, "raw_w2_00", 12288)
         raw["w2_01"] = placed([P, PACK, KP], F32, "raw_w2_01", 20480)
         raw["w2_11"] = placed([P, PACK, KP], F32, "raw_w2_11", 4096)
@@ -249,7 +256,7 @@ def tile_list_scenario_cashflow_values_kernel(
 
         def leave(bank, b0, u0, u1, ch0, ch1, on_vector=False):
             width = (ch1 - ch0) * CH
-            result = kept([P, u1 - u0, width], F32, f"result{u0}{ch0}")
+            result = lined([P, u1 - u0, width], F32, f"result{u0}{ch0}", 1)
             if on_vector:
                 nc.vector.tensor_tensor(
                     out=result[:],

from contextlib import ExitStack

import concourse.mybir as mybir
from concourse.masks import make_identity

K, M, H, N, T, T2, S = 512, 1024, 1024, 512, 2048, 4096, 1024
FLOPS = 2 * S * (K * H + M * H + H * N)

F32 = mybir.dt.float32
BF16 = mybir.dt.bfloat16
I32 = mybir.dt.int32
U32 = mybir.dt.uint32
U16 = mybir.dt.uint16
U8 = mybir.dt.uint8
FP8X4 = mybir.dt.float8_e4m3fn_x4
FP4X4 = mybir.dt.float4_e2m1fn_x4
EXP = mybir.ActivationFunctionType.Exp
COPY = mybir.ActivationFunctionType.Copy
MULT = mybir.AluOpType.mult

P = 128
QUADRANT = 32
SCALE_ROWS = 4
BLOCKS = 16
PACK = 4
KP = P * PACK
I32_BYTES = 4
LIST_GROUP = 16
HALF = 512
CH = 128
LINE = 4
PAIR = 2
OUT_TILES = N // P
AHEAD = (0, 1, 2, 3, 6, 7)
PARKED = ((0, 6), (0, 7), (1, 4))
W1_CUT = 320
LAST_CUT = 192
CASH_BANKS = {0: (0, 1, 2, 3, 4, 5, 6, 7), 1: (6, 7, 2, 4, 3, 6, 3, 4)}
BANKS = 8
DISCOUNT_BANKS = 3

W2_PIECES = {"w2_00": (0, 0), "w2_01": (1, 0), "w2_10": (0, 1), "w2_11": (1, 1)}
PIECES = ["w1_0", "w1_1", *W2_PIECES]

RUNS = {0: [(0, 2), (2, 4), (4, 6), (6, 7), (7, 8)], 1: [(0, 2), (2, 4), (4, 5), (5, 6), (6, 7), (7, 8)]}
VALUES_AT = {(0, 4): 0, (0, 7): 2048, (1, 4): 2048}
CODES_AT = {(0, 1): 4096, (0, 3): 22528}


def tile_list_scenario_cashflow_values_kernel(
    tc, tab_words, tab_scales, offs, tab2_words, tab2_scales, offs2, w1, b1, w2, w4_words, w4_scales, fx, out
):
    nc = tc.nc
    with ExitStack() as ctx:
        keep = ctx.enter_context(tc.tile_pool(name="keep", bufs=1))
        ring = ctx.enter_context(tc.tile_pool(name="ring", bufs=3))
        shared = ctx.enter_context(tc.tile_pool(name="shared", bufs=1))
        moved = ctx.enter_context(tc.tile_pool(name="moved", bufs=1))
        psum = ctx.enter_context(tc.psum_pool(name="psum", bufs=1))

        def kept(shape, dtype, name):
            return keep.tile(shape, dtype, name=name, align_bytes=256)

        taken = []

        def lined(shape, dtype, name, size):
            taken.append(size)
            return moved.tile(shape, dtype, name=name, align_bytes=1024, offset=1024 * (sum(taken) - size))

        def placed(shape, dtype, name, offset):
            return shared.tile(shape, dtype, name=name, align_bytes=1024, offset=offset)

        idx = kept([P, S // LIST_GROUP], U16, "idx")
        idx2 = kept([P, S // LIST_GROUP], U16, "idx2")
        curve_words = lined([P, T], I32, "curve_words", 8)
        curve_scales = lined([P, T // I32_BYTES], I32, "curve_scales", 2)
        cash_words = [lined([P, T2], I32, f"cash_words{g}", 16) for g in range(2)]
        cash_scales = lined([P, T2 // I32_BYTES], I32, "cash_scales", 4)
        shift_words = [lined([P, 2 * N // I32_BYTES], I32, f"shift_words{a}", 1) for a in range(2)]
        shift_scales = lined([P, 2, N // I32_BYTES], I32, "shift_scales", 1)
        bias = kept([P, 2, PACK], F32, "bias")
        rate = kept([P, OUT_TILES], F32, "rate")
        v_words = kept([P, S], U32, "v_words")
        v2_words = [kept([P, S], U32, f"v2_words{g}") for g in range(2)]
        rows = lined([P, 2 * S], U8, "rows", 2)
        planes = [lined([P, S // I32_BYTES], I32, "planes0", 1), lined([P, 2 * S // I32_BYTES], I32, "planes1", 2)]

        raw_w1 = lined([P, PACK, H], F32, "raw_w1", 16)
        raw = {name: lined([P, PACK, KP], F32, "raw_" + name, 8) for name in ("w2_10",)}
        raw["w2_00"] = placed([P, PACK, KP], F32, "raw_w2_00", 12288)
        raw["w2_01"] = placed([P, PACK, KP], F32, "raw_w2_01", 20480)
        raw["w2_11"] = placed([P, PACK, KP], F32, "raw_w2_11", 4096)
        raw["w1_0"], raw["w1_1"] = raw_w1[:, :, 0:KP], raw_w1[:, :, KP:H]
        w_codes = {name: kept([P, KP], U32, "codes_" + name) for name in PIECES}
        w_scales = {name: kept([P, KP], U8, "scales_" + name) for name in PIECES}
        disc = {(a, hf): kept([P, PACK, HALF], F32, f"disc{a}{hf}") for a in range(2) for hf in range(2)}
        h_codes = {}
        h_scales = {(a, pr): kept([P, 2 * CH], U8, f"h_scales{a}{pr}") for a in range(2) for pr in range(4)}
        rounded, values, cash_bank, out_bank, woven, parked = {}, {}, {}, {}, {}, {}

        nc.vector.memset(cash_scales[:], 0)
        nc.vector.memset(curve_scales[:], 0)
        nc.vector.memset(planes[1][:], 0)
        nc.vector.memset(planes[0][:], 0)
        nc.vector.memset(shift_scales[:], 0)
        bias_rows = kept([P, KP], F32, "values10")
        identity = kept([P, P], F32, "values12")
        nc.vector.memset(bias_rows[:], 0.0)
        nc.vector.memset(identity[:], 0.0)
        make_identity(nc, identity[:], nomemset=True)

        def load_words(tile, words, t0, t1):
            nc.sync.dma_start(out=tile[:, t0:t1], in_=words[:, t0:t1, :].rearrange("p t i -> p (t i)").bitcast(I32))

        def load_w2(name, c0=0, c1=KP):
            g, a = W2_PIECES[name]
            src = w2[g * KP : (g + 1) * KP, a * KP + c0 : a * KP + c1]
            nc.sync.dma_start(out=raw[name][:, :, c0:c1], in_=src.rearrange("(p j) c -> p j c", j=PACK))

        def load_shift_scales(s0, s1):
            for s in range(s0, s1):
                nc.sync.dma_start(
                    out=shift_scales[s:P:QUADRANT, :, :],
                    in_=w4_scales.bitcast(I32)[:, s:BLOCKS:SCALE_ROWS, :].rearrange("a q n -> q a n"),
                )

        def place_scales(g):
            c0 = 0 if g == 1 else S // I32_BYTES
            for s in range(SCALE_ROWS):
                nc.sync.dma_start(
                    out=planes[g][SCALE_ROWS * (g + 1) + s : P : QUADRANT, :],
                    in_=rows[:].bitcast(I32)[4 * (BLOCKS * g + s) : 4 * BLOCKS * (g + 1) : 4 * SCALE_ROWS, c0:],
                )

        def gather(dst, window, offsets, j0, j1):
            nc.vector.tensor_copy(dst[:, j0:j1], window.indirect(offsets[:, j0 // LIST_GROUP : j1 // LIST_GROUP]))

        def round_piece(name, copy, cuts=(0, KP), grouped=None):
            if grouped is None:
                grouped = ring.tile([P, PACK, P, PACK], BF16, name="grouped", align_bytes=256)
            for c0, c1 in zip(cuts[:-1], cuts[1:]):
                copy(
                    out=grouped[:, :, c0 // PACK : c1 // PACK, :].rearrange("p t m j -> p m j t"),
                    in_=raw[name][:, :, c0:c1].rearrange("p j (m t) -> p m j t", t=PACK),
                )
            rounded[name] = grouped

        def quantize_piece(name, calls=1):
            for i in range(calls):
                t0, t1 = i * PACK // calls, (i + 1) * PACK // calls
                nc.vector.quantize_mx(
                    out=w_codes[name][:, t0 * P : t1 * P].bitcast(FP8X4),
                    scales=w_scales[name][:, t0 * P : t1 * P],
                    in_=rounded[name][:, t0:t1, :, :].rearrange("p t m j -> p (t m j)"),
                )

        def discount(a, hf, turn):
            name = f"w1_{a}"
            cols = slice(hf * HALF, (hf + 1) * HALF)
            for t in range(PACK):
                bank = psum.tile([P, HALF], F32, name=f"bank{BANKS - 1 - (15 - turn * PACK - t) % DISCOUNT_BANKS}")
                nc.tensor.matmul_mx(
                    out=bank[:],
                    lhsT=w_codes[name][:, t * P : (t + 1) * P].bitcast(FP8X4),
                    lhsT_scale=w_scales[name][:, t * P : (t + 1) * P],
                    rhs=v_words[:, cols].bitcast(FP8X4),
                    rhs_scale=planes[1][:].bitcast(U8)[2 * SCALE_ROWS : P, cols],
                    start=True,
                    stop=True,
                )
                nc.scalar.activation(out=disc[a, hf][:, t, :], in_=bank[:], func=EXP, bias=bias[:, a, t : t + 1])

        def cashflow_pass(a, ch, g, t0=0, t1=PACK, first=0):
            cols = slice(ch * CH, (ch + 1) * CH)
            if (g, t0) == (first, 0):
                cash_bank[a, ch] = psum.tile([P, PACK, CH], F32, name=f"bank{CASH_BANKS[a][ch]}")
            name = f"w2_{a}{g}"
            for t in range(t0, t1):
                nc.tensor.matmul_mx(
                    out=cash_bank[a, ch][:, t, :],
                    lhsT=w_codes[name][:, t * P : (t + 1) * P].bitcast(FP8X4),
                    lhsT_scale=w_scales[name][:, t * P : (t + 1) * P],
                    rhs=v2_words[g][:, cols].bitcast(FP8X4),
                    rhs_scale=planes[g][:].bitcast(U8)[SCALE_ROWS * (g + 1) : P, g * S :][:, cols],
                    start=(g == first and t == 0),
                    stop=(g != first and t == PACK - 1),
                )

        def cashflow(a, ch):
            for g in range(2):
                cashflow_pass(a, ch, g)

        def weave(a, ch):
            hf, j0 = divmod(ch * CH, HALF)
            woven[a, ch] = placed([P, CH, PACK], F32, f"woven{a}{ch}", 12288 + 2048 * PARKED.index((a, ch)))
            nc.vector.tensor_copy(
                out=woven[a, ch][:].rearrange("p (c i) t -> p c t i", i=LINE),
                in_=disc[a, hf][:, :, j0 : j0 + CH].rearrange("p t (c i) -> p c t i", i=LINE),
            )

        def park(a, ch):
            parked[a, ch] = placed([P, CH, PACK], F32, f"parked{a}{ch}", 20480 + 2048 * PARKED.index((a, ch)))
            nc.scalar.copy(out=parked[a, ch][:], in_=cash_bank[a, ch][:].rearrange("p t j -> p j t"))

        def present_value(a, ch):
            hf, j0 = divmod(ch * CH, HALF)
            first, end = [run for run in RUNS[a] if run[0] <= ch < run[1]][0]
            if ch == first:
                shape = [P, (end - first) * CH, PACK]
                if (a, first) in VALUES_AT:
                    values[a, first] = placed(shape, BF16, f"values{a}{first}", VALUES_AT[a, first])
                else:
                    values[a, first] = kept(shape, BF16, f"values{a}{first}")
            i0 = (ch - first) * CH
            if (a, ch) in parked:
                nc.gpsimd.tensor_tensor(
                    out=values[a, first][:, i0 : i0 + CH, :], in0=parked[a, ch][:], in1=woven[a, ch][:], op=MULT
                )
                return
            nc.vector.tensor_tensor(
                out=values[a, first][:, i0 : i0 + CH, :].rearrange("p (c i) t -> p c t i", i=PAIR),
                in0=cash_bank[a, ch][:].rearrange("p t (c i) -> p c t i", i=PAIR),
                in1=disc[a, hf][:, :, j0 : j0 + CH].rearrange("p t (c i) -> p c t i", i=PAIR),
                op=MULT,
            )

        def quantize_run(a, first):
            pr, j0 = divmod(first * CH, 2 * CH)
            if (a, pr) not in h_codes:
                if (a, pr) in CODES_AT:
                    h_codes[a, pr] = placed([P, 2 * CH], U32, f"h_codes{a}{pr}", CODES_AT[a, pr])
                else:
                    h_codes[a, pr] = kept([P, 2 * CH], U32, f"h_codes{a}{pr}")
            j1 = j0 + values[a, first].shape[1]
            nc.vector.quantize_mx(
                out=h_codes[a, pr][:, j0:j1].bitcast(FP8X4),
                scales=h_scales[a, pr][:, j0:j1],
                in_=values[a, first][:].rearrange("p j t -> p (j t)"),
            )

        def scenario_pass(a, bank, u0, u1, ch0, ch1):
            width = (ch1 - ch0) * CH
            if a == 0:
                out_bank[u0, ch0] = psum.tile([P, u1 - u0, width], F32, name=f"bank{bank}")
            pr = ch0 // 2
            for u in range(u0, u1):
                nc.tensor.matmul_mx(
                    out=out_bank[u0, ch0][:, u - u0, :],
                    lhsT=shift_words[a][:].bitcast(U8)[:, 2 * P * u : 2 * P * (u + 1)].bitcast(FP4X4),
                    lhsT_scale=shift_scales[:, a, :].bitcast(U8)[:, P * u : P * (u + 1)],
                    rhs=h_codes[a, pr][:].bitcast(FP8X4),
                    rhs_scale=h_scales[a, pr][:],
                    start=(a == 0 and u == u0),
                    stop=(a == 1 and u == u1 - 1),
                )

        def leave(bank, b0, u0, u1, ch0, ch1, on_vector=False):
            width = (ch1 - ch0) * CH
            result = lined([P, u1 - u0, width], F32, f"result{u0}{ch0}", 1)
            if on_vector:
                nc.vector.tensor_tensor(
                    out=result[:],
                    in0=bank[:, b0 : b0 + u1 - u0, :],
                    in1=rate[:, u0:u1].unsqueeze(2).to_broadcast([P, u1 - u0, width]),
                    op=MULT,
                )
            else:
                for u in range(u0, u1):
                    nc.scalar.activation(
                        out=result[:, u - u0, :], in_=bank[:, b0 + u - u0, :], func=COPY, scale=rate[:, u : u + 1]
                    )
            store(result[:], u0, u1, ch0 * CH, ch1 * CH)

        def open_pair(ch, banks):
            for i in range(2):
                scenario_pass(0, banks[i], 2 * i, 2 * i + 2, ch, ch + 2)

        def close_pair(ch):
            for i in range(2):
                scenario_pass(1, None, 2 * i, 2 * i + 2, ch, ch + 2)
                for u in range(2 * i, 2 * i + 2):
                    leave(out_bank[2 * i, ch], u - 2 * i, u, u + 1, ch, ch + 2)

        def store(result, u0, u1, j0, j1):
            nc.sync.dma_start(out=out[u0 * P : u1 * P, j0:j1].rearrange("(u p) j -> p u j", p=P), in_=result)

        load_words(curve_words, tab_words[0], 0, 3 * T // 4)
        nc.sync.dma_start(idx2[:], offs2)
        nc.sync.dma_start(idx[:], offs)
        nc.sync.dma_start(out=cash_scales[0:P:4, :], in_=tab2_scales.bitcast(I32).rearrange("g q t -> (g q) t"))
        nc.sync.dma_start(out=curve_scales[4 * BLOCKS : P : 4, :], in_=tab_scales[0].bitcast(I32))
        load_words(curve_words, tab_words[0], 3 * T // 4, T)
        nc.sync.dma_start(out=raw_w1[:], in_=w1.rearrange("(p j) c -> p j c", j=PACK))
        nc.sync.dma_start(out=bias_rows[0:2, :], in_=b1.rearrange("(a c) -> a c", a=2))
        load_words(cash_words[1], tab2_words[1], 0, 5 * T2 // 8)

        gather(rows[:, S:], cash_scales[:].bitcast(U8), idx2, 0, S)
        gather(rows[:, 0:S], curve_scales[:].bitcast(U8), idx, 0, S)
        gather(v_words, curve_words[:].bitcast(U32), idx, 0, S)

        place_scales(1)
        load_words(cash_words[1], tab2_words[1], 5 * T2 // 8, T2)
        load_w2("w2_01")
        place_scales(0)
        load_w2("w2_00")
        load_words(cash_words[0], tab2_words[0], 0, T2)
        load_shift_scales(0, 2)
        load_w2("w2_10")
        load_shift_scales(2, SCALE_ROWS)
        nc.sync.dma_start(out=shift_words[0][:], in_=w4_words[0].bitcast(I32))
        load_w2("w2_11", 0, KP // 2)
        load_w2("w2_11", KP // 2, KP)
        nc.sync.dma_start(out=shift_words[1][:], in_=w4_words[1].bitcast(I32))
        with nc.allow_non_contiguous_dma(reason="one rate to a partition and output tile"):
            nc.sync.dma_start(out=rate[:], in_=fx.rearrange("(u p) -> p u", p=P))

        turned = psum.tile([P, PACK, P], F32, name="bank0")
        for t in range(PACK):
            nc.tensor.transpose(turned[:, t, :], bias_rows[:, t:KP:PACK], identity[:])
        round_piece("w1_0", nc.scalar.copy)
        nc.scalar.copy(out=bias[:], in_=turned[:, :, 0:2].rearrange("p t a -> p a t"))
        both = ring.tile([P, PACK, P, PACK], BF16, name="grouped", align_bytes=256)
        round_piece("w1_1", nc.vector.tensor_copy, (0, W1_CUT), both)
        quantize_piece("w1_0")
        round_piece("w1_1", nc.scalar.copy, (W1_CUT, KP), both)
        quantize_piece("w1_1")
        for turn, (a, hf) in enumerate(((0, 1), (1, 0), (1, 1), (0, 0))):
            discount(a, hf, turn)

        gather(v2_words[1], cash_words[1][:].bitcast(U32), idx2, 0, S)
        round_piece("w2_01", nc.vector.tensor_copy)
        quantize_piece("w2_01")
        round_piece("w2_00", nc.vector.tensor_copy)
        quantize_piece("w2_00")
        for a, ch in PARKED:
            weave(a, ch)
        for ch0, ch1 in ((6, 8), (0, 2), (2, 6)):
            gather(v2_words[0], cash_words[0][:].bitcast(U32), idx2, ch0 * CH, ch1 * CH)

        for ch in AHEAD:
            cashflow_pass(0, ch, 1, first=1)
        for ch in (6, 7, 0, 1, 2, 3):
            cashflow_pass(0, ch, 0, first=1)
        cashflow(0, 4)
        cashflow(0, 5)
        park(0, 6)
        park(0, 7)
        present_value(0, 6)
        round_piece("w2_10", nc.scalar.copy)
        last_rounded = placed([P, PACK, P, PACK], BF16, "last_rounded", 0)
        round_piece("w2_11", nc.scalar.copy, (LAST_CUT, KP // 2, KP), last_rounded)
        for ch in range(3):
            present_value(0, ch)
        quantize_run(0, 0)
        open_pair(0, (0, 1))
        present_value(0, 3)
        quantize_piece("w2_10", calls=2)
        for t0 in (0, 2):
            for ch in range(2):
                cashflow_pass(1, ch, 0, t0, t0 + 2)
        cashflow_pass(1, 2, 0)
        cashflow_pass(1, 4, 0)
        round_piece("w2_11", nc.vector.tensor_copy, (0, LAST_CUT), last_rounded)
        quantize_piece("w2_11", calls=2)
        for t0 in (0, 2):
            for ch in range(2):
                cashflow_pass(1, ch, 1, t0, t0 + 2)
        cashflow_pass(1, 4, 1)
        park(1, 4)
        cashflow_pass(1, 2, 1)


        quantize_run(0, 2)
        present_value(0, 7)
        present_value(0, 4)
        cashflow(1, 3)
        present_value(1, 0)
        cashflow(1, 5)
        present_value(1, 1)
        quantize_run(0, 6)
        quantize_run(0, 7)
        quantize_run(1, 0)
        close_pair(0)
        cashflow(1, 6)
        present_value(1, 4)
        present_value(1, 2)
        open_pair(2, (7, 2))
        present_value(1, 3)
        cashflow(1, 7)
        present_value(0, 5)
        quantize_run(1, 2)
        close_pair(2)
        present_value(1, 5)
        for u, bank in ((0, 1), (1, 6)):
            scenario_pass(0, bank, u, u + 1, 6, 8)
        quantize_run(0, 4)
        open_pair(4, (5, 0))
        quantize_run(1, 4)
        quantize_run(1, 5)
        close_pair(4)
        present_value(1, 6)
        for u, bank in ((2, 7), (3, 3)):
            scenario_pass(0, bank, u, u + 1, 6, 8)
        present_value(1, 7)
        quantize_run(1, 6)
        quantize_run(1, 7)
        for u in range(OUT_TILES):
            scenario_pass(1, None, u, u + 1, 6, 8)
            leave(out_bank[u, 6], 0, u, u + 1, 6, 8, on_vector=(u % 2 == 1))
